import numpy as np
import ml_dtypes


def mxq(x, axis, fmt="e4m3"):
    dtype, down = {"e4m3": (ml_dtypes.float8_e4m3fn, 7), "e5m2": (ml_dtypes.float8_e5m2, 14)}[fmt]
    v = np.moveaxis(np.asarray(x, np.float32).astype(ml_dtypes.bfloat16).astype(np.float64), axis, -1)
    blocks = v.reshape(v.shape[:-1] + (-1, 32))
    amax = np.abs(blocks).max(-1, keepdims=True)
    byte = np.maximum(np.where(amax > 0, np.frexp(amax)[1] - 1 + 127, 0) - down, 1)
    scale = np.exp2(byte - 127.0)
    codes = (blocks / scale).astype(np.float32).astype(dtype).astype(np.float64)
    return np.moveaxis((codes * scale).reshape(v.shape), -1, axis)


WIDE = False


def mx_kscale(k):
    if not WIDE:
        return np.ones(k)
    levels = np.array([10, -10, 5, -5, 0])
    if k % 512:
        return np.exp2(np.random.permutation(np.resize(levels, k // 32))).repeat(32)
    a = np.empty((k // 512, 16))
    for p in range(k // 512):
        a[p, :8] = np.random.permutation(np.resize(levels, 8))
        for g in range(8):
            far = levels[np.abs(levels - a[p, g]) >= 10]
            a[p, g + 8] = far[np.random.randint(len(far))]
    return np.exp2(a.ravel()).repeat(32)


def f64(x):
    return np.asarray(x).astype(np.float64)


def striped(idx):
    return np.tile(idx.reshape(-1, 16).T, (8, 1)).astype(np.uint16)


def unstriped(offs):
    return offs[:16].T.reshape(-1).astype(np.int64)


E2M1 = np.array([0.0, 0.5, 1.0, 1.5, 2.0, 3.0, 4.0, 6.0, -0.0, -0.5, -1.0, -1.5, -2.0, -3.0, -4.0, -6.0])


def pack_weight(w, fmt):
    k, n = w.shape
    w = f64(np.asarray(w, np.float32).astype(ml_dtypes.bfloat16)).reshape(k // 32, 32, n)
    amax = np.abs(w).max(1)
    if fmt == "e4m3":
        byte = np.frexp(amax)[1] - 1 + 127 - 7
    else:
        mant, ex = np.frexp(amax / 6.0)
        byte = np.where(mant > 0.5, ex, ex - 1) + 127
    byte = np.clip(np.where(amax > 0, byte, 1), 1, 254)
    scaled = (w * np.exp2(127.0 - byte)[:, None, :]).reshape(k, n).astype(np.float32)
    by_word = np.ascontiguousarray(scaled.reshape(k // 512, 128, 4, n).transpose(0, 1, 3, 2))
    if fmt == "e4m3":
        words = by_word.astype(ml_dtypes.float8_e4m3fn).view(np.uint8)
    else:
        c = by_word.astype(ml_dtypes.float4_e2m1fn).view(np.uint8) & 0xF
        words = (c[..., 0::2] | (c[..., 1::2] << 4)).reshape(k // 512, 128, 2 * n)
    return np.ascontiguousarray(words), np.ascontiguousarray(byte.astype(np.uint8).reshape(k // 512, 16, n))


def unpack_weight(words, scales, fmt):
    g, _, n = scales.shape
    words = np.ascontiguousarray(words).reshape(g, 128, n, -1)
    if fmt == "e4m3":
        vals = words.view(ml_dtypes.float8_e4m3fn).astype(np.float64)
    else:
        nib = np.empty((g, 128, n, 4), np.uint8)
        nib[..., 0::2] = words & 0xF
        nib[..., 1::2] = words >> 4
        vals = E2M1[nib]
    vals = vals * np.repeat(np.exp2(scales.astype(np.float64) - 127.0), 8, axis=1)[..., None]
    return vals.transpose(0, 1, 3, 2).reshape(g * 512, n)


def gelu(v):
    return 0.5 * v * (1.0 + np.tanh(np.sqrt(2.0 / np.pi) * (v + 0.044715 * v**3)))


def bf(x):
    return np.asarray(x, np.float32).astype(ml_dtypes.bfloat16)


def planes(Y):
    n, m = Y.shape
    b = f64(bf(Y)).reshape(n // 32, 32, m)
    amax = np.abs(b).max(1)
    byte = np.clip(np.where(amax > 0, np.frexp(amax)[1] - 1 + 127 - 7, 1), 1, 254)
    codes = (b * np.exp2(127.0 - byte)[:, None, :]).reshape(n, m).astype(np.float32).astype(ml_dtypes.float8_e4m3fn).view(np.uint8)
    words = codes.reshape(n // 512, 128, 4, m).transpose(0, 1, 3, 2)
    return np.ascontiguousarray(words), np.ascontiguousarray(byte.astype(np.uint8).reshape(n // 512, 16, m))


K, H, N, T, S, T2 = 1536, 1024, 512, 2048, 512, 1024

def setup_inputs():
    n = np.random.standard_normal
    s = mx_kscale(K)[:, None]
    u = mx_kscale(H)[:, None]
    tab_words, tab_scales = pack_weight(n((K, T)) * s, "e4m3")
    wd_words, wd_scales = pack_weight(n((K, H)) / s / np.sqrt(K), "e2m1")
    return {
        "tab_words": tab_words, "tab_scales": tab_scales,
        "offs": striped(np.random.permutation(T)[:S]),
        "offs2": striped(np.random.permutation(T2)[:S]),
        "offs3": striped(np.random.permutation(T2)[:S]),
        "wa": (n((K, H)) / s / np.sqrt(K)).astype(np.float32),
        "wd_words": wd_words, "wd_scales": wd_scales,
        "wg1": np.exp(0.3 * n((128, S))).astype(np.float32),
        "wg2": np.exp(0.3 * n((128, S))).astype(np.float32),
        "gain": (np.exp(0.3 * n(H)) * u[:, 0]).astype(np.float32),
        "res": (0.7 * n((H, T2)) * u).astype(np.float32),
        "wo": (n((H, N)) * np.exp(0.8 * n((1, N))) / u / np.sqrt(H)).astype(np.float32),
    }

def reference(tab_words, tab_scales, offs, offs2, offs3, wa, wd_words, wd_scales,
              wg1, wg2, gain, res, wo):
    v = unpack_weight(tab_words, tab_scales, "e4m3")[:, unstriped(offs)]
    h1 = mxq(f64(wa), 0, "e4m3").T @ v
    h2 = unpack_weight(wd_words, wd_scales, "e2m1").T @ v
    pageA = np.zeros((H, T2))
    pageA[:, unstriped(offs2)] = np.tile(f64(wg1), (H // 128, 1)) * h1
    pageB = np.zeros((H, T2))
    pageB[:, unstriped(offs3)] = np.tile(f64(wg2), (H // 128, 1)) * h2
    both = pageA / (1.0 + np.exp(-pageA)) + pageB / (1.0 + np.exp(-pageB))
    z = both * f64(gain)[:, None] + f64(res)
    y = mxq(f64(wo), 0, "e4m3").T @ mxq(z, 0, "e4m3")
    words, scales = planes(y)
    return y, words, scales

@@ -1,0 +1,342 @@
+from contextlib import ExitStack
+
+import concourse.mybir as mybir
+from concourse.masks import make_identity
+
+K, H, N, T, S, T2 = 1536, 1024, 512, 2048, 512, 1024
+FLOPS = 2 * (2 * K * H * S + H * N * T2)
+
+F32 = mybir.dt.float32
+BF16 = mybir.dt.bfloat16
+I32 = mybir.dt.int32
+U32 = mybir.dt.uint32
+U16 = mybir.dt.uint16
+U8 = mybir.dt.uint8
+E4M3 = mybir.dt.float8_e4m3fn_x4
+E2M1 = mybir.dt.float4_e2m1fn_x4
+ACT = mybir.ActivationFunctionType
+MULT = mybir.AluOpType.mult
+
+P = 128
+PACK = 4
+PASS = P * PACK
+KP = K // PASS
+RP = H // PASS
+TILES = H // P
+BANK = 512
+HALVES = T2 // BANK
+WA_COLS = 256
+WA_CHUNKS = H // WA_COLS
+LEAD = 4
+HOLD = 8
+RES_BUFS = 3
+WD_FIRST = 2
+GAIN_ON_SCALAR = (11, 12, 13, 14)
+WO_STEPS = (9, 11)
+QUART = 256
+
+
+def step_order():
+    steps = [("dep", i) for i in range(LEAD)]
+    for c in range(WA_CHUNKS):
+        steps.extend([("arr", 2 * c), ("arr", 2 * c + 1), ("dep", LEAD + c)])
+    return steps
+
+
+def tile_list_parish_migration_pages_kernel(
+    tc, tab_words, tab_scales, offs, offs2, offs3, wa, wd_words, wd_scales,
+    wg1, wg2, gain, res, wo, out_0, out_1, out_2,
+):
+    nc = tc.nc
+    with ExitStack() as ctx:
+        keep = ctx.enter_context(tc.tile_pool(name="keep", bufs=1))
+        psum = ctx.enter_context(tc.psum_pool(name="psum", bufs=1))
+
+        def sb(name, shape, dtype, tag=None):
+            return keep.tile(shape, dtype, name=name, tag=tag or name, align_bytes=64)
+
+        banks = [psum.tile([P, BANK], F32, name=f"bank{b}") for b in range(8)]
+        h_banks, sum_banks, word_banks = banks[0:2], banks[2:6], banks[6:8]
+
+        list_t = sb("list_t", [P, S // 16], U16)
+        lists = {"arr": sb("list_a", [P, S // 16], U16), "dep": sb("list_d", [P, S // 16], U16)}
+        table = [sb(f"table{a}", [P, T], I32, tag=f"big{a}") for a in range(KP)]
+        table_sc = sb("table_sc", [P, KP, T], U8)
+        wd_sc = sb("wd_sc", [P, KP, H], U8)
+        wd_a = sb("wd_a", [P, KP, WD_FIRST * 2 * P], U8)
+        wd_b = sb("wd_b", [P, KP, (TILES - WD_FIRST) * 2 * P], U8)
+        wg = {"arr": sb("wg_a", [P, S], F32), "dep": sb("wg_d", [P, S], F32)}
+        wa_raw = [[sb(f"wa_raw{c}_{a}", [P, PACK * WA_COLS], F32) for a in range(KP)] for c in range(WA_CHUNKS)]
+        res_t = [sb(f"res{b}", [P, T2], F32) for b in range(RES_BUFS)]
+        pages = {kind: [sb(f"page_{kind}{b}", [P, T2], F32) for b in range(2)] for kind in ("arr", "dep")}
+        ident = sb("ident", [P, P], F32)
+        gain_rows = sb("gain_rows", [P, P], F32)
+        gain_t = sb("gain_t", [P, TILES], F32)
+        warm = sb("warm", [P, 2], F32)
+
+        def load_scale_rows(queue, dst, src):
+            for q in range(4):
+                queue.dma_start(
+                    out=dst[32 * q : 32 * q + 4, :, :].bitcast(I32),
+                    in_=src[:, 4 * q : 4 * q + 4, :].rearrange("a r c -> r a c").bitcast(I32),
+                )
+
+        def load_table(a):
+            nc.sync.dma_start(out=table[a][:], in_=tab_words[a].rearrange("p t i -> p (t i)").bitcast(I32))
+
+        def load_wa(c):
+            for a in range(KP):
+                rows = wa[a * PASS : (a + 1) * PASS, c * WA_COLS : (c + 1) * WA_COLS]
+                nc.sync.dma_start(
+                    out=wa_raw[c][a][:].rearrange("p (j c) -> p j c", j=PACK),
+                    in_=rows.rearrange("(p j) c -> p j c", j=PACK),
+                )
+
+        def load_res(i):
+            nc.sync.dma_start(out=res_t[i % RES_BUFS][:], in_=res[i * P : (i + 1) * P, :])
+
+        nc.vector.memset(table_sc[:].rearrange("p a c -> p (a c)").bitcast(I32), 0)
+        nc.vector.memset(wd_sc[:].rearrange("p a c -> p (a c)").bitcast(I32), 0)
+        nc.gpsimd.memset(warm[:, 0:1], 0.0)
+        nc.scalar.activation(warm[:, 1:2], warm[:, 0:1], ACT.Silu)
+        nc.gpsimd.memset(gain_rows[:], 0.0)
+        make_identity(nc, ident[:])
+        nc.gpsimd.dma_start(out=gain_rows[0:TILES, :], in_=gain.rearrange("(i p) -> i p", p=P))
+        load_scale_rows(nc.gpsimd, wd_sc, wd_scales)
+        for kind in ("dep", "arr"):
+            for page in pages[kind]:
+                nc.gpsimd.memset(page[:], 0.0)
+
+        nc.sync.dma_start(list_t[:], offs)
+        nc.sync.dma_start(lists["dep"][:], offs3)
+        nc.sync.dma_start(lists["arr"][:], offs2)
+        load_scale_rows(nc.scalar, table_sc, tab_scales)
+        for a in range(KP):
+            load_table(a)
+        wd_view = wd_words.rearrange("a p c -> p a c")
+        nc.sync.dma_start(out=wd_a[:].bitcast(I32), in_=wd_view[:, :, : WD_FIRST * 2 * P].bitcast(I32))
+        nc.sync.dma_start(out=wg["dep"][:], in_=wg2)
+        nc.sync.dma_start(out=wd_b[:].bitcast(I32), in_=wd_view[:, :, WD_FIRST * 2 * P :].bitcast(I32))
+        load_wa(0)
+        nc.sync.dma_start(out=wg["arr"][:], in_=wg1)
+        load_wa(1)
+        load_res(0)
+        load_res(1)
+        load_wa(2)
+        load_res(2)
+        load_wa(3)
+        wo_raw = [sb(f"wo_raw{g}", [P, PACK, N], F32, tag=f"big{g}") for g in range(RP)]
+
+        v_words = [sb(f"v_words{a}", [P, S], U32) for a in range(KP)]
+        v_sc = [sb(f"v_sc{a}", [P, S], U8) for a in range(KP)]
+        for a in range(KP):
+            nc.vector.tensor_copy(v_sc[a][:], table_sc[:, a, :].indirect(list_t[:]))
+            nc.vector.tensor_copy(v_words[a][:], table[a][:].bitcast(U32).indirect(list_t[:]))
+        for g in range(RP):
+            nc.sync.dma_start(
+                out=wo_raw[g][:], in_=wo[g * PASS : (g + 1) * PASS, :].rearrange("(p j) n -> p j n", j=PACK)
+            )
+
+        nc.tensor.transpose(word_banks[0][:, 0:P], gain_rows[:], ident[:])
+        nc.scalar.copy(gain_t[:], word_banks[0][:, 0:TILES])
+
+        wa_bf = [sb(f"wa_bf{a}", [P, PACK * WA_COLS], BF16) for a in range(KP)]
+        wa_codes = [[sb(f"wa_codes{c}_{a}", [P, WA_COLS], U32) for a in range(KP)] for c in range(WA_CHUNKS)]
+        wa_sc = [[sb(f"wa_sc{c}_{a}", [P, WA_COLS], U8) for a in range(KP)] for c in range(WA_CHUNKS)]
+        held = [sb(f"held{b}", [P, T2], F32) for b in range(HOLD)]
+        silu_first = sb("silu_first", [P, T2], F32)
+        z_rows = [[sb(f"z_rows{g}_{hb}", [P, 4, 2, 2 * P], BF16) for hb in range(HALVES)] for g in range(RP)]
+        z_in = [sb(f"z_in{hb}", [P, PACK * BANK], BF16) for hb in range(HALVES)]
+        z_codes = [[sb(f"z_codes{g}_{hb}", [P, BANK], U32) for hb in range(HALVES)] for g in range(RP)]
+        z_sc = [[sb(f"z_sc{g}_{hb}", [P, BANK], U8) for hb in range(HALVES)] for g in range(RP)]
+        wo_codes = [sb(f"wo_codes{g}", [P, N], U32) for g in range(RP)]
+        wo_sc = [sb(f"wo_sc{g}", [P, N], U8) for g in range(RP)]
+
+        def quantize_wa(c):
+            for a in range(KP):
+                nc.scalar.copy(
+                    wa_bf[a][:].rearrange("p (c i j) -> p c j i", i=4, j=PACK),
+                    wa_raw[c][a][:].rearrange("p (j c i) -> p c j i", i=4, j=PACK),
+                )
+            for a in range(KP):
+                nc.vector.quantize_mx(out=wa_codes[c][a][:].bitcast(E4M3), scales=wa_sc[c][a][:], in_=wa_bf[a][:])
+
+        def quantize_wo(g):
+            nc.scalar.copy(
+                z_in[g][:].rearrange("p (t m j) -> p m j t", t=PACK, j=PACK),
+                wo_raw[g][:].rearrange("p j (m t) -> p m j t", t=PACK),
+            )
+            nc.vector.quantize_mx(out=wo_codes[g][:].bitcast(E4M3), scales=wo_sc[g][:], in_=z_in[g][:])
+
+        steps = step_order()
+        where = {step: j for j, step in enumerate(steps)}
+
+        def h_stage(j):
+            return held[(j - 1) % HOLD][:, 0:S]
+
+        def silu_tile(j):
+            if j == 0:
+                return silu_first
+            c, a = divmod((j - 1) % (WA_CHUNKS * KP), KP)
+            return wa_raw[c][KP - 1 - a]
+
+        def gained(j):
+            return silu_tile(j) if j in GAIN_ON_SCALAR else held[j % HOLD]
+
+        def product(j):
+            kind, i = steps[j]
+            bank = h_banks[j % 2]
+            for a in range(KP):
+                if kind == "arr":
+                    c, col = divmod(i * P, WA_COLS)
+                    lhs = wa_codes[c][a][:, col : col + P].bitcast(E4M3)
+                    lhs_sc = wa_sc[c][a][:, col : col + P]
+                else:
+                    src, n = (wd_a, i) if i < WD_FIRST else (wd_b, i - WD_FIRST)
+                    lhs = src[:, a, n * 2 * P : (n + 1) * 2 * P].bitcast(E2M1)
+                    lhs_sc = wd_sc[:, a, i * P : (i + 1) * P]
+                nc.tensor.matmul_mx(
+                    out=bank[:], lhsT=lhs, lhsT_scale=lhs_sc, rhs=v_words[a][:].bitcast(E4M3),
+                    rhs_scale=v_sc[a][:], start=(a == 0), stop=(a == KP - 1),
+                )
+            nc.scalar.copy(h_stage(j), bank[:])
+
+        def scatter(j):
+            kind, i = steps[j]
+            page = pages[kind][i % 2]
+            nc.vector.tensor_tensor(page[:].indirect(lists[kind][:]), h_stage(j), wg[kind][:], MULT)
+
+        def activate(j, cols):
+            kind, i = steps[j]
+            s_tile = silu_tile(j)
+            nc.scalar.activation(s_tile[:, cols], pages[kind][i % 2][:, cols], ACT.Silu)
+            dst = gained(j)[:, cols]
+            if j in GAIN_ON_SCALAR:
+                nc.scalar.activation(dst, s_tile[:, cols], ACT.Copy, scale=gain_t[:, i : i + 1])
+            else:
+                nc.vector.tensor_scalar(dst, s_tile[:, cols], gain_t[:, i : i + 1], None, MULT)
+
+        def add_term(i, hb, src, first, last):
+            bank = sum_banks[2 * (i % 2) + hb]
+            for b in range(4):
+                m0 = (4 * hb + b) * P
+                nc.tensor.matmul(
+                    bank[:, b * P : (b + 1) * P], src[:, m0 : m0 + P], ident[:],
+                    start=(first and b == 0), stop=(last and b == 3), is_transpose=True,
+                )
+
+        def open_sum(i):
+            early = min(where[("arr", i)], where[("dep", i)])
+            for hb in range(HALVES):
+                add_term(i, hb, res_t[i % RES_BUFS], True, False)
+                add_term(i, hb, gained(early), False, False)
+            if i + RES_BUFS < TILES:
+                load_res(i + RES_BUFS)
+
+        def close_sum(i, hb):
+            late = max(where[("arr", i)], where[("dep", i)])
+            add_term(i, hb, gained(late), False, True)
+            g, quarter = divmod(i, 4)
+            nc.scalar.copy(
+                z_rows[g][hb][:, :, :, 64 * quarter : 64 * (quarter + 1)].rearrange("p b u (q e) -> p b u q e", e=2),
+                sum_banks[2 * (i % 2) + hb][:].rearrange("p (b q u e) -> p b u q e", b=4, u=2, e=2),
+            )
+
+        def interleave_z(g, q, bank, copy):
+            hb, pair = divmod(q, 2)
+            words = z_rows[g][hb][:].bitcast(F32)
+            for b in range(2):
+                for u in range(2):
+                    col = (2 * b + u) * P
+                    nc.tensor.transpose(bank[:, col : col + P], words[:, 2 * pair + b, u, :], ident[:])
+            copy(
+                z_in[hb][:].bitcast(F32)[:, pair * BANK : (pair + 1) * BANK].rearrange("p (b m u) -> p b m u", b=2, u=2),
+                bank[:].rearrange("p (b u m) -> p b m u", b=2, u=2),
+            )
+
+        def quantize_z(g, hb, lo, hi):
+            nc.vector.quantize_mx(
+                out=z_codes[g][hb][:, lo:hi].bitcast(E4M3), scales=z_sc[g][hb][:, lo:hi],
+                in_=z_in[hb][:, PACK * lo : PACK * hi],
+            )
+
+        y_banks = [banks[0:2], banks[2:4], banks[6:8], banks[4:6]]
+
+        def y_pass(g, q):
+            hb, pair = divmod(q, 2)
+            cols = slice(pair * QUART, (pair + 1) * QUART)
+            for t in range(PACK):
+                nc.tensor.matmul_mx(
+                    out=y_banks[q][t // 2][:, (t % 2) * QUART : (t % 2 + 1) * QUART],
+                    lhsT=wo_codes[g][:, t * P : (t + 1) * P].bitcast(E4M3),
+                    lhsT_scale=wo_sc[g][:, t * P : (t + 1) * P], rhs=z_codes[g][hb][:, cols].bitcast(E4M3),
+                    rhs_scale=z_sc[g][hb][:, cols], start=(g == 0 and t % 2 == 0), stop=(g == RP - 1 and t % 2 == 1),
+                )
+
+        whole = slice(0, T2)
+        last = len(steps) - 1
+        closes = {max(where[("arr", i)], where[("dep", i)]): i for i in range(TILES)}
+        product(0)
+        product(1)
+        scatter(0)
+        for j in range(last):
+            if j % KP == 1 and j // KP < WA_CHUNKS:
+                quantize_wa(j // KP)
+            if j + 2 <= last:
+                product(j + 2)
+            scatter(j + 1)
+            if j in closes:
+                open_sum(closes[j])
+            activate(j, whole)
+            if j in closes:
+                for hb in range(HALVES):
+                    close_sum(closes[j], hb)
+                if closes[j] == 3:
+                    for q in range(4):
+                        interleave_z(0, q, word_banks[q % 2], nc.scalar.copy)
+                    for hb in range(HALVES):
+                        quantize_z(0, hb, 0, BANK)
+            if j in WO_STEPS:
+                quantize_wo(WO_STEPS.index(j))
+
+        open_sum(TILES - 1)
+        y_pass(0, 0)
+        y_pass(0, 1)
+        for hb in range(HALVES):
+            activate(last, slice(hb * BANK, (hb + 1) * BANK))
+        for hb in range(HALVES):
+            close_sum(TILES - 1, hb)
+        tail_banks = [banks[6], banks[7], banks[4], banks[5]]
+        for q in range(4):
+            interleave_z(1, q, tail_banks[q], nc.vector.tensor_copy if q % 2 == 0 else nc.scalar.copy)
+        y_view = out_0.rearrange("(p t) m -> p t m", t=PACK)
+        codes_view = out_1[0].rearrange("p m t -> p (m t)").bitcast(I32)
+        y_sc = sb("y_sc", [P, T2], U8)
+        y_codes = [sb(f"y_codes{q}", [P, QUART], U32) for q in range(4)]
+        for q in range(4):
+            quantize_z(1, q // 2, (q % 2) * QUART, (q % 2 + 1) * QUART)
+            if q >= 2:
+                y_pass(0, q)
+            y_pass(1, q)
+        for q in range(4):
+            cols = slice(q * QUART, (q + 1) * QUART)
+            y_sb = held[q]
+            y_bf = z_rows[0][q // 2][:].rearrange("p b u w -> p (b u w)")[:, (q % 2) * PACK * QUART : (q % 2 + 1) * PACK * QUART]
+            for s in range(2):
+                half = y_sb[:, s * BANK : (s + 1) * BANK]
+                if q == 3 and s == 1:
+                    nc.vector.tensor_copy(half, y_banks[q][s][:])
+                else:
+                    nc.scalar.copy(half, y_banks[q][s][:])
+            nc.sync.dma_start(out=y_view[:, :, cols], in_=y_sb[:].rearrange("p (t m) -> p t m", t=PACK))
+            nc.vector.tensor_copy(
+                y_bf.rearrange("p (c i t) -> p c t i", i=4, t=PACK),
+                y_sb[:].rearrange("p (t c i) -> p c t i", i=4, t=PACK),
+            )
+            nc.vector.quantize_mx(out=y_codes[q][:].bitcast(E4M3), scales=y_sc[:, cols], in_=y_bf)
+            nc.sync.dma_start(out=codes_view[:, cols], in_=y_codes[q][:].bitcast(I32))
+        for q in range(4):
+            queue = nc.sync if q % 2 == 0 else nc.scalar
+            queue.dma_start(
+                out=out_2[0, 4 * q : 4 * q + 4, :].bitcast(I32), in_=y_sc[32 * q : 32 * q + 4, :].bitcast(I32)
+            )

@@ -31,9 +31,11 @@ LEAD = 4
 HOLD = 8
 RES_BUFS = 3
 WD_FIRST = 2
-GAIN_ON_SCALAR = (11, 12, 13, 14)
-WO_STEPS = (9, 11)
+GAIN_ON_SCALAR = (0, 1, 12, 13, 14)
+WO_STEPS = (6, 8)
+Z0_STEPS = (13, 15)
 QUART = 256
+SUM_LAG = 2
 
 
 def step_order():
@@ -65,7 +67,7 @@ def tile_list_parish_migration_pages_kernel(
         wd_sc = sb("wd_sc", [P, KP, H], U8)
         wd_a = sb("wd_a", [P, KP, WD_FIRST * 2 * P], U8)
         wd_b = sb("wd_b", [P, KP, (TILES - WD_FIRST) * 2 * P], U8)
-        wg = {"arr": sb("wg_a", [P, S], F32), "dep": sb("wg_d", [P, S], F32)}
+        wg = {kind: sb("wg_" + kind, [P, S], F32) for kind in ("arr", "dep")}
         wa_raw = [[sb(f"wa_raw{c}_{a}", [P, PACK * WA_COLS], F32) for a in range(KP)] for c in range(WA_CHUNKS)]
         res_t = [sb(f"res{b}", [P, T2], F32) for b in range(RES_BUFS)]
         pages = {kind: [sb(f"page_{kind}{b}", [P, T2], F32) for b in range(2)] for kind in ("arr", "dep")}
@@ -110,12 +112,12 @@ def tile_list_parish_migration_pages_kernel(
         nc.sync.dma_start(list_t[:], offs)
         nc.sync.dma_start(lists["dep"][:], offs3)
         nc.sync.dma_start(lists["arr"][:], offs2)
+        nc.sync.dma_start(out=wg["dep"][:], in_=wg2)
         load_scale_rows(nc.scalar, table_sc, tab_scales)
         for a in range(KP):
             load_table(a)
         wd_view = wd_words.rearrange("a p c -> p a c")
         nc.sync.dma_start(out=wd_a[:].bitcast(I32), in_=wd_view[:, :, : WD_FIRST * 2 * P].bitcast(I32))
-        nc.sync.dma_start(out=wg["dep"][:], in_=wg2)
         nc.sync.dma_start(out=wd_b[:].bitcast(I32), in_=wd_view[:, :, WD_FIRST * 2 * P :].bitcast(I32))
         load_wa(0)
         nc.sync.dma_start(out=wg["arr"][:], in_=wg1)
@@ -127,11 +129,13 @@ def tile_list_parish_migration_pages_kernel(
         load_wa(3)
         wo_raw = [sb(f"wo_raw{g}", [P, PACK, N], F32, tag=f"big{g}") for g in range(RP)]
 
-        v_words = [sb(f"v_words{a}", [P, S], U32) for a in range(KP)]
         v_sc = [sb(f"v_sc{a}", [P, S], U8) for a in range(KP)]
         for a in range(KP):
             nc.vector.tensor_copy(v_sc[a][:], table_sc[:, a, :].indirect(list_t[:]))
-            nc.vector.tensor_copy(v_words[a][:], table[a][:].bitcast(U32).indirect(list_t[:]))
+        v_all = sb("v_words", [P, KP * S], U32, tag="table_sc")
+        v_words = [v_all[:, a * S : (a + 1) * S] for a in range(KP)]
+        for a in range(KP):
+            nc.vector.tensor_copy(v_words[a], table[a][:].bitcast(U32).indirect(list_t[:]))
         for g in range(RP):
             nc.sync.dma_start(
                 out=wo_raw[g][:], in_=wo[g * PASS : (g + 1) * PASS, :].rearrange("(p j) n -> p j n", j=PACK)
@@ -144,10 +148,10 @@ def tile_list_parish_migration_pages_kernel(
         wa_codes = [[sb(f"wa_codes{c}_{a}", [P, WA_COLS], U32) for a in range(KP)] for c in range(WA_CHUNKS)]
         wa_sc = [[sb(f"wa_sc{c}_{a}", [P, WA_COLS], U8) for a in range(KP)] for c in range(WA_CHUNKS)]
         held = [sb(f"held{b}", [P, T2], F32) for b in range(HOLD)]
-        silu_first = sb("silu_first", [P, T2], F32)
+        silu_first = sb("silu_first", [P, T2], F32, tag="big2")
         z_rows = [[sb(f"z_rows{g}_{hb}", [P, 4, 2, 2 * P], BF16) for hb in range(HALVES)] for g in range(RP)]
         z_in = [sb(f"z_in{hb}", [P, PACK * BANK], BF16) for hb in range(HALVES)]
-        z_codes = [[sb(f"z_codes{g}_{hb}", [P, BANK], U32) for hb in range(HALVES)] for g in range(RP)]
+        z_codes = {(1, hb): sb(f"z_codes1_{hb}", [P, BANK], U32) for hb in range(HALVES)}
         z_sc = [[sb(f"z_sc{g}_{hb}", [P, BANK], U8) for hb in range(HALVES)] for g in range(RP)]
         wo_codes = [sb(f"wo_codes{g}", [P, N], U32) for g in range(RP)]
         wo_sc = [sb(f"wo_sc{g}", [P, N], U8) for g in range(RP)]
@@ -162,11 +166,14 @@ def tile_list_parish_migration_pages_kernel(
                 nc.vector.quantize_mx(out=wa_codes[c][a][:].bitcast(E4M3), scales=wa_sc[c][a][:], in_=wa_bf[a][:])
 
         def quantize_wo(g):
-            nc.scalar.copy(
-                z_in[g][:].rearrange("p (t m j) -> p m j t", t=PACK, j=PACK),
-                wo_raw[g][:].rearrange("p j (m t) -> p m j t", t=PACK),
-            )
-            nc.vector.quantize_mx(out=wo_codes[g][:].bitcast(E4M3), scales=wo_sc[g][:], in_=z_in[g][:])
+            for s in range(2):
+                stage = wa_bf[(2 * g + s) % KP]
+                nc.scalar.copy(
+                    stage[:].rearrange("p (t m j) -> p m j t", t=2, j=PACK),
+                    wo_raw[g][:].rearrange("p j (m t) -> p m j t", t=PACK)[:, :, :, 2 * s : 2 * s + 2],
+                )
+                cols = slice(2 * s * P, 2 * (s + 1) * P)
+                nc.vector.quantize_mx(out=wo_codes[g][:, cols].bitcast(E4M3), scales=wo_sc[g][:, cols], in_=stage[:])
 
         steps = step_order()
         where = {step: j for j, step in enumerate(steps)}
@@ -174,11 +181,16 @@ def tile_list_parish_migration_pages_kernel(
         def h_stage(j):
             return held[(j - 1) % HOLD][:, 0:S]
 
+        free_raw = [wa_raw[c][a] for c in range(WA_CHUNKS) for a in (2, 0)] + [wa_raw[c][1] for c in range(WA_CHUNKS)]
+        silu_tiles = {0: silu_first}
+
         def silu_tile(j):
-            if j == 0:
-                return silu_first
-            c, a = divmod((j - 1) % (WA_CHUNKS * KP), KP)
-            return wa_raw[c][KP - 1 - a]
+            if j not in silu_tiles:
+                if j in WO_STEPS:
+                    silu_tiles[j] = sb(f"silu{j}", [P, T2], F32, tag=f"big{WO_STEPS.index(j)}")
+                else:
+                    silu_tiles[j] = free_raw[(j - 1) % len(free_raw)]
+            return silu_tiles[j]
 
         def gained(j):
             return silu_tile(j) if j in GAIN_ON_SCALAR else held[j % HOLD]
@@ -196,7 +208,7 @@ def tile_list_parish_migration_pages_kernel(
                     lhs = src[:, a, n * 2 * P : (n + 1) * 2 * P].bitcast(E2M1)
                     lhs_sc = wd_sc[:, a, i * P : (i + 1) * P]
                 nc.tensor.matmul_mx(
-                    out=bank[:], lhsT=lhs, lhsT_scale=lhs_sc, rhs=v_words[a][:].bitcast(E4M3),
+                    out=bank[:], lhsT=lhs, lhsT_scale=lhs_sc, rhs=v_words[a].bitcast(E4M3),
                     rhs_scale=v_sc[a][:], start=(a == 0), stop=(a == KP - 1),
                 )
             nc.scalar.copy(h_stage(j), bank[:])
@@ -256,11 +268,11 @@ def tile_list_parish_migration_pages_kernel(
 
         def quantize_z(g, hb, lo, hi):
             nc.vector.quantize_mx(
-                out=z_codes[g][hb][:, lo:hi].bitcast(E4M3), scales=z_sc[g][hb][:, lo:hi],
+                out=z_codes[(g, hb)][:, lo:hi].bitcast(E4M3), scales=z_sc[g][hb][:, lo:hi],
                 in_=z_in[hb][:, PACK * lo : PACK * hi],
             )
 
-        y_banks = [banks[0:2], banks[2:4], banks[6:8], banks[4:6]]
+        y_banks = [banks[0:2], banks[6:8], banks[2:4], banks[4:6]]
 
         def y_pass(g, q):
             hb, pair = divmod(q, 2)
@@ -269,36 +281,43 @@ def tile_list_parish_migration_pages_kernel(
                 nc.tensor.matmul_mx(
                     out=y_banks[q][t // 2][:, (t % 2) * QUART : (t % 2 + 1) * QUART],
                     lhsT=wo_codes[g][:, t * P : (t + 1) * P].bitcast(E4M3),
-                    lhsT_scale=wo_sc[g][:, t * P : (t + 1) * P], rhs=z_codes[g][hb][:, cols].bitcast(E4M3),
+                    lhsT_scale=wo_sc[g][:, t * P : (t + 1) * P], rhs=z_codes[(g, hb)][:, cols].bitcast(E4M3),
                     rhs_scale=z_sc[g][hb][:, cols], start=(g == 0 and t % 2 == 0), stop=(g == RP - 1 and t % 2 == 1),
                 )
 
         whole = slice(0, T2)
         last = len(steps) - 1
         closes = {max(where[("arr", i)], where[("dep", i)]): i for i in range(TILES)}
-        product(0)
-        product(1)
-        scatter(0)
-        for j in range(last):
-            if j % KP == 1 and j // KP < WA_CHUNKS:
-                quantize_wa(j // KP)
-            if j + 2 <= last:
-                product(j + 2)
-            scatter(j + 1)
-            if j in closes:
-                open_sum(closes[j])
-            activate(j, whole)
+        def finish_sum(j):
             if j in closes:
                 for hb in range(HALVES):
                     close_sum(closes[j], hb)
                 if closes[j] == 3:
                     for q in range(4):
                         interleave_z(0, q, word_banks[q % 2], nc.scalar.copy)
-                    for hb in range(HALVES):
-                        quantize_z(0, hb, 0, BANK)
+
+        product(0)
+        product(1)
+        scatter(0)
+        for j in range(last):
+            if j % 2 == 1 and j // 2 < WA_CHUNKS:
+                quantize_wa(j // 2)
             if j in WO_STEPS:
                 quantize_wo(WO_STEPS.index(j))
+            if j + 2 <= last:
+                product(j + 2)
+            scatter(j + 1)
+            if j + 1 in Z0_STEPS:
+                hb = Z0_STEPS.index(j + 1)
+                z_codes[(0, hb)] = sb(f"z_codes0_{hb}", [P, BANK], U32, tag=("wg_dep" if j + 1 == last else f"held{j % HOLD}"))
+                quantize_z(0, hb, 0, BANK)
+            activate(j, whole)
+            finish_sum(j - SUM_LAG)
+            if j in closes:
+                open_sum(closes[j])
 
+        for j in range(last - SUM_LAG, last):
+            finish_sum(j)
         open_sum(TILES - 1)
         y_pass(0, 0)
         y_pass(0, 1)
@@ -306,7 +325,7 @@ def tile_list_parish_migration_pages_kernel(
             activate(last, slice(hb * BANK, (hb + 1) * BANK))
         for hb in range(HALVES):
             close_sum(TILES - 1, hb)
-        tail_banks = [banks[6], banks[7], banks[4], banks[5]]
+        tail_banks = banks[2:6]
         for q in range(4):
             interleave_z(1, q, tail_banks[q], nc.vector.tensor_copy if q % 2 == 0 else nc.scalar.copy)
         y_view = out_0.rearrange("(p t) m -> p t m", t=PACK)
@@ -320,14 +339,11 @@ def tile_list_parish_migration_pages_kernel(
             y_pass(1, q)
         for q in range(4):
             cols = slice(q * QUART, (q + 1) * QUART)
-            y_sb = held[q]
+            y_sb = wa_raw[q][1]
             y_bf = z_rows[0][q // 2][:].rearrange("p b u w -> p (b u w)")[:, (q % 2) * PACK * QUART : (q % 2 + 1) * PACK * QUART]
             for s in range(2):
                 half = y_sb[:, s * BANK : (s + 1) * BANK]
-                if q == 3 and s == 1:
-                    nc.vector.tensor_copy(half, y_banks[q][s][:])
-                else:
-                    nc.scalar.copy(half, y_banks[q][s][:])
+                nc.scalar.copy(half, y_banks[q][s][:])
             nc.sync.dma_start(out=y_view[:, :, cols], in_=y_sb[:].rearrange("p (t m) -> p t m", t=PACK))
             nc.vector.tensor_copy(
                 y_bf.rearrange("p (c i t) -> p c t i", i=4, t=PACK),

@@ -31,8 +31,8 @@ LEAD = 4
 HOLD = 8
 RES_BUFS = 3
 WD_FIRST = 2
-GAIN_ON_SCALAR = (0, 1, 12, 13, 14)
-WO_STEPS = (6, 8)
+GAIN_ON_SCALAR = (1, 3, 12, 13, 14)
+WO_STEPS = (7, 9)
 Z0_STEPS = (13, 15)
 QUART = 256
 SUM_LAG = 2
@@ -65,12 +65,12 @@ def tile_list_parish_migration_pages_kernel(
         table = [sb(f"table{a}", [P, T], I32, tag=f"big{a}") for a in range(KP)]
         table_sc = sb("table_sc", [P, KP, T], U8)
         wd_sc = sb("wd_sc", [P, KP, H], U8)
-        wd_a = sb("wd_a", [P, KP, WD_FIRST * 2 * P], U8)
+        wd_a = [sb(f"wd_a{i}", [P, KP, 2 * P], U8) for i in range(WD_FIRST)]
         wd_b = sb("wd_b", [P, KP, (TILES - WD_FIRST) * 2 * P], U8)
         wg = {kind: sb("wg_" + kind, [P, S], F32) for kind in ("arr", "dep")}
         wa_raw = [[sb(f"wa_raw{c}_{a}", [P, PACK * WA_COLS], F32) for a in range(KP)] for c in range(WA_CHUNKS)]
         res_t = [sb(f"res{b}", [P, T2], F32) for b in range(RES_BUFS)]
-        pages = {kind: [sb(f"page_{kind}{b}", [P, T2], F32) for b in range(2)] for kind in ("arr", "dep")}
+        pages = {"arr": [], "dep": [sb("page_dep0", [P, T2], F32)]}
         ident = sb("ident", [P, P], F32)
         gain_rows = sb("gain_rows", [P, P], F32)
         gain_t = sb("gain_t", [P, TILES], F32)
@@ -104,22 +104,21 @@ def tile_list_parish_migration_pages_kernel(
         nc.gpsimd.memset(gain_rows[:], 0.0)
         make_identity(nc, ident[:])
         nc.gpsimd.dma_start(out=gain_rows[0:TILES, :], in_=gain.rearrange("(i p) -> i p", p=P))
+        load_scale_rows(nc.gpsimd, table_sc, tab_scales)
         load_scale_rows(nc.gpsimd, wd_sc, wd_scales)
-        for kind in ("dep", "arr"):
-            for page in pages[kind]:
-                nc.gpsimd.memset(page[:], 0.0)
+        nc.vector.memset(pages["dep"][0][:], 0.0)
 
         nc.sync.dma_start(list_t[:], offs)
-        nc.sync.dma_start(lists["dep"][:], offs3)
-        nc.sync.dma_start(lists["arr"][:], offs2)
-        nc.sync.dma_start(out=wg["dep"][:], in_=wg2)
-        load_scale_rows(nc.scalar, table_sc, tab_scales)
         for a in range(KP):
             load_table(a)
         wd_view = wd_words.rearrange("a p c -> p a c")
-        nc.sync.dma_start(out=wd_a[:].bitcast(I32), in_=wd_view[:, :, : WD_FIRST * 2 * P].bitcast(I32))
+        nc.sync.dma_start(out=wd_a[0][:].bitcast(I32), in_=wd_view[:, :, : 2 * P].bitcast(I32))
+        nc.sync.dma_start(lists["dep"][:], offs3)
+        nc.sync.dma_start(out=wg["dep"][:], in_=wg2)
+        nc.sync.dma_start(out=wd_a[1][:].bitcast(I32), in_=wd_view[:, :, 2 * P : 4 * P].bitcast(I32))
         nc.sync.dma_start(out=wd_b[:].bitcast(I32), in_=wd_view[:, :, WD_FIRST * 2 * P :].bitcast(I32))
         load_wa(0)
+        nc.sync.dma_start(lists["arr"][:], offs2)
         nc.sync.dma_start(out=wg["arr"][:], in_=wg1)
         load_wa(1)
         load_res(0)
@@ -132,8 +131,9 @@ def tile_list_parish_migration_pages_kernel(
         v_sc = [sb(f"v_sc{a}", [P, S], U8) for a in range(KP)]
         for a in range(KP):
             nc.vector.tensor_copy(v_sc[a][:], table_sc[:, a, :].indirect(list_t[:]))
-        v_all = sb("v_words", [P, KP * S], U32, tag="table_sc")
-        v_words = [v_all[:, a * S : (a + 1) * S] for a in range(KP)]
+        v_first = sb("v_first", [P, S], U32)
+        v_rest = sb("v_rest", [P, (KP - 1) * S], U32, tag="table_sc")
+        v_words = [v_first[:]] + [v_rest[:, a * S : (a + 1) * S] for a in range(KP - 1)]
         for a in range(KP):
             nc.vector.tensor_copy(v_words[a], table[a][:].bitcast(U32).indirect(list_t[:]))
         for g in range(RP):
@@ -144,11 +144,10 @@ def tile_list_parish_migration_pages_kernel(
         nc.tensor.transpose(word_banks[0][:, 0:P], gain_rows[:], ident[:])
         nc.scalar.copy(gain_t[:], word_banks[0][:, 0:TILES])
 
-        wa_bf = [sb(f"wa_bf{a}", [P, PACK * WA_COLS], BF16) for a in range(KP)]
+        h_first = sb("h_first", [P, S], F32)
         wa_codes = [[sb(f"wa_codes{c}_{a}", [P, WA_COLS], U32) for a in range(KP)] for c in range(WA_CHUNKS)]
         wa_sc = [[sb(f"wa_sc{c}_{a}", [P, WA_COLS], U8) for a in range(KP)] for c in range(WA_CHUNKS)]
         held = [sb(f"held{b}", [P, T2], F32) for b in range(HOLD)]
-        silu_first = sb("silu_first", [P, T2], F32, tag="big2")
         z_rows = [[sb(f"z_rows{g}_{hb}", [P, 4, 2, 2 * P], BF16) for hb in range(HALVES)] for g in range(RP)]
         z_in = [sb(f"z_in{hb}", [P, PACK * BANK], BF16) for hb in range(HALVES)]
         z_codes = {(1, hb): sb(f"z_codes1_{hb}", [P, BANK], U32) for hb in range(HALVES)}
@@ -159,37 +158,37 @@ def tile_list_parish_migration_pages_kernel(
         def quantize_wa(c):
             for a in range(KP):
                 nc.scalar.copy(
-                    wa_bf[a][:].rearrange("p (c i j) -> p c j i", i=4, j=PACK),
+                    wa_bf[a].rearrange("p (c i j) -> p c j i", i=4, j=PACK),
                     wa_raw[c][a][:].rearrange("p (j c i) -> p c j i", i=4, j=PACK),
                 )
             for a in range(KP):
-                nc.vector.quantize_mx(out=wa_codes[c][a][:].bitcast(E4M3), scales=wa_sc[c][a][:], in_=wa_bf[a][:])
+                nc.vector.quantize_mx(out=wa_codes[c][a][:].bitcast(E4M3), scales=wa_sc[c][a][:], in_=wa_bf[a])
 
         def quantize_wo(g):
             for s in range(2):
                 stage = wa_bf[(2 * g + s) % KP]
                 nc.scalar.copy(
-                    stage[:].rearrange("p (t m j) -> p m j t", t=2, j=PACK),
+                    stage.rearrange("p (t m j) -> p m j t", t=2, j=PACK),
                     wo_raw[g][:].rearrange("p j (m t) -> p m j t", t=PACK)[:, :, :, 2 * s : 2 * s + 2],
                 )
                 cols = slice(2 * s * P, 2 * (s + 1) * P)
-                nc.vector.quantize_mx(out=wo_codes[g][:, cols].bitcast(E4M3), scales=wo_sc[g][:, cols], in_=stage[:])
+                nc.vector.quantize_mx(out=wo_codes[g][:, cols].bitcast(E4M3), scales=wo_sc[g][:, cols], in_=stage)
 
         steps = step_order()
         where = {step: j for j, step in enumerate(steps)}
 
         def h_stage(j):
-            return held[(j - 1) % HOLD][:, 0:S]
+            return h_first[:] if j == 0 else held[(j - 1) % HOLD][:, 0:S]
 
         free_raw = [wa_raw[c][a] for c in range(WA_CHUNKS) for a in (2, 0)] + [wa_raw[c][1] for c in range(WA_CHUNKS)]
-        silu_tiles = {0: silu_first}
+        silu_tiles = {}
 
         def silu_tile(j):
             if j not in silu_tiles:
                 if j in WO_STEPS:
                     silu_tiles[j] = sb(f"silu{j}", [P, T2], F32, tag=f"big{WO_STEPS.index(j)}")
                 else:
-                    silu_tiles[j] = free_raw[(j - 1) % len(free_raw)]
+                    silu_tiles[j] = free_raw[j % len(free_raw)]
             return silu_tiles[j]
 
         def gained(j):
@@ -204,7 +203,7 @@ def tile_list_parish_migration_pages_kernel(
                     lhs = wa_codes[c][a][:, col : col + P].bitcast(E4M3)
                     lhs_sc = wa_sc[c][a][:, col : col + P]
                 else:
-                    src, n = (wd_a, i) if i < WD_FIRST else (wd_b, i - WD_FIRST)
+                    src, n = (wd_a[i], 0) if i < WD_FIRST else (wd_b, i - WD_FIRST)
                     lhs = src[:, a, n * 2 * P : (n + 1) * 2 * P].bitcast(E2M1)
                     lhs_sc = wd_sc[:, a, i * P : (i + 1) * P]
                 nc.tensor.matmul_mx(
@@ -218,15 +217,19 @@ def tile_list_parish_migration_pages_kernel(
             page = pages[kind][i % 2]
             nc.vector.tensor_tensor(page[:].indirect(lists[kind][:]), h_stage(j), wg[kind][:], MULT)
 
-        def activate(j, cols):
+        def activate(j):
             kind, i = steps[j]
             s_tile = silu_tile(j)
-            nc.scalar.activation(s_tile[:, cols], pages[kind][i % 2][:, cols], ACT.Silu)
-            dst = gained(j)[:, cols]
-            if j in GAIN_ON_SCALAR:
-                nc.scalar.activation(dst, s_tile[:, cols], ACT.Copy, scale=gain_t[:, i : i + 1])
-            else:
-                nc.vector.tensor_scalar(dst, s_tile[:, cols], gain_t[:, i : i + 1], None, MULT)
+            split = j in GAIN_ON_SCALAR or j == len(steps) - 1
+            parts = [slice(hb * BANK, (hb + 1) * BANK) for hb in range(HALVES)] if split else [slice(0, T2)]
+            for cols in parts:
+                nc.scalar.activation(s_tile[:, cols], pages[kind][i % 2][:, cols], ACT.Silu)
+            for cols in parts:
+                dst = gained(j)[:, cols]
+                if j in GAIN_ON_SCALAR:
+                    nc.scalar.activation(dst, s_tile[:, cols], ACT.Copy, scale=gain_t[:, i : i + 1])
+                else:
+                    nc.vector.tensor_scalar(dst, s_tile[:, cols], gain_t[:, i : i + 1], None, MULT)
 
         def add_term(i, hb, src, first, last):
             bank = sum_banks[2 * (i % 2) + hb]
@@ -285,7 +288,6 @@ def tile_list_parish_migration_pages_kernel(
                     rhs_scale=z_sc[g][hb][:, cols], start=(g == 0 and t % 2 == 0), stop=(g == RP - 1 and t % 2 == 1),
                 )
 
-        whole = slice(0, T2)
         last = len(steps) - 1
         closes = {max(where[("arr", i)], where[("dep", i)]): i for i in range(TILES)}
         def finish_sum(j):
@@ -297,10 +299,16 @@ def tile_list_parish_migration_pages_kernel(
                         interleave_z(0, q, word_banks[q % 2], nc.scalar.copy)
 
         product(0)
+        stage_all = sb("stage_all", [P, KP * PACK * WA_COLS], BF16, tag="wd_a0")
+        wa_bf = [stage_all[:, a * PACK * WA_COLS : (a + 1) * PACK * WA_COLS] for a in range(KP)]
         product(1)
         scatter(0)
+        for kind, tag in (("dep", "big2"), ("arr", "wd_a1"), ("arr", "h_first")):
+            page = sb("page_" + tag, [P, T2], F32, tag=tag)
+            nc.gpsimd.memset(page[:], 0.0)
+            pages[kind].append(page)
         for j in range(last):
-            if j % 2 == 1 and j // 2 < WA_CHUNKS:
+            if j % 2 == 0 and j // 2 < WA_CHUNKS:
                 quantize_wa(j // 2)
             if j in WO_STEPS:
                 quantize_wo(WO_STEPS.index(j))
@@ -311,7 +319,7 @@ def tile_list_parish_migration_pages_kernel(
                 hb = Z0_STEPS.index(j + 1)
                 z_codes[(0, hb)] = sb(f"z_codes0_{hb}", [P, BANK], U32, tag=("wg_dep" if j + 1 == last else f"held{j % HOLD}"))
                 quantize_z(0, hb, 0, BANK)
-            activate(j, whole)
+            activate(j)
             finish_sum(j - SUM_LAG)
             if j in closes:
                 open_sum(closes[j])
@@ -321,8 +329,7 @@ def tile_list_parish_migration_pages_kernel(
         open_sum(TILES - 1)
         y_pass(0, 0)
         y_pass(0, 1)
-        for hb in range(HALVES):
-            activate(last, slice(hb * BANK, (hb + 1) * BANK))
+        activate(last)
         for hb in range(HALVES):
             close_sum(TILES - 1, hb)
         tail_banks = banks[2:6]
@@ -344,7 +351,7 @@ def tile_list_parish_migration_pages_kernel(
             for s in range(2):
                 half = y_sb[:, s * BANK : (s + 1) * BANK]
                 nc.scalar.copy(half, y_banks[q][s][:])
-            nc.sync.dma_start(out=y_view[:, :, cols], in_=y_sb[:].rearrange("p (t m) -> p t m", t=PACK))
+                nc.sync.dma_start(out=y_view[:, 2 * s : 2 * s + 2, cols], in_=half.rearrange("p (t m) -> p t m", t=2))
             nc.vector.tensor_copy(
                 y_bf.rearrange("p (c i t) -> p c t i", i=4, t=PACK),
                 y_sb[:].rearrange("p (t c i) -> p c t i", i=4, t=PACK),

@@ -16,6 +16,7 @@ E4M3 = mybir.dt.float8_e4m3fn_x4
 E2M1 = mybir.dt.float4_e2m1fn_x4
 ACT = mybir.ActivationFunctionType
 MULT = mybir.AluOpType.mult
+ADD = mybir.AluOpType.add
 
 P = 128
 PACK = 4
@@ -25,24 +26,28 @@ RP = H // PASS
 TILES = H // P
 BANK = 512
 HALVES = T2 // BANK
-WA_COLS = 256
-WA_CHUNKS = H // WA_COLS
-LEAD = 4
-HOLD = 8
-RES_BUFS = 3
-WD_FIRST = 2
-GAIN_ON_SCALAR = (1, 3, 12, 13, 14)
-WO_STEPS = (7, 9)
-Z0_STEPS = (13, 15)
 QUART = 256
-SUM_LAG = 2
+CHUNKS = T2 // QUART
+WA_COLS = 256
+WA_CHUNKS = PASS // WA_COLS
+SCALE_ROWS = 16
+RES_RING = 4
+H_RING = 3
+AHEAD = 2
+WIDE_RING = 8
+GAIN_RUN = 13
+CAST_STEPS = (0, 11)
+WIDE_STEP = 4
+NEEDS = {1: 0, 4: 2, 8: 4, 12: 10}
+WEIGHED_FIRST = 2
+QUANTIZE_STEPS = (0, 2, 10, 13)
+Z0_STEP = 11
+DEAL_STEP = 4
 
 
 def step_order():
-    steps = [("dep", i) for i in range(LEAD)]
-    for c in range(WA_CHUNKS):
-        steps.extend([("arr", 2 * c), ("arr", 2 * c + 1), ("dep", LEAD + c)])
-    return steps
+    steps = [(kind, 2 * c + h) for c in range(WA_CHUNKS) for kind in ("dep", "arr") for h in range(2)]
+    return steps + [(kind, i) for kind in ("dep", "arr") for i in range(PACK, TILES)]
 
 
 def tile_list_parish_migration_pages_kernel(
@@ -57,306 +62,393 @@ def tile_list_parish_migration_pages_kernel(
         def sb(name, shape, dtype, tag=None):
             return keep.tile(shape, dtype, name=name, tag=tag or name, align_bytes=64)
 
+        made = {}
+
+        def later(name, shape, dtype, tag):
+            if name not in made:
+                made[name] = sb(name, shape, dtype, tag=tag)
+            return made[name]
+
         banks = [psum.tile([P, BANK], F32, name=f"bank{b}") for b in range(8)]
         h_banks, sum_banks, word_banks = banks[0:2], banks[2:6], banks[6:8]
 
         list_t = sb("list_t", [P, S // 16], U16)
         lists = {"arr": sb("list_a", [P, S // 16], U16), "dep": sb("list_d", [P, S // 16], U16)}
         table = [sb(f"table{a}", [P, T], I32, tag=f"big{a}") for a in range(KP)]
-        table_sc = sb("table_sc", [P, KP, T], U8)
+        table_sc = sb("table_sc", [P, T], U8)
+        picked_sc = sb("picked_sc", [P, S], U8)
+        v_sc = sb("v_sc", [P, KP, S], U8)
         wd_sc = sb("wd_sc", [P, KP, H], U8)
-        wd_a = [sb(f"wd_a{i}", [P, KP, 2 * P], U8) for i in range(WD_FIRST)]
-        wd_b = sb("wd_b", [P, KP, (TILES - WD_FIRST) * 2 * P], U8)
+        wd_raw = [sb(f"wd_raw{g}", [P, KP, 2 * PASS], U8) for g in range(RP)]
         wg = {kind: sb("wg_" + kind, [P, S], F32) for kind in ("arr", "dep")}
+        wg_dealt = {kind: [sb(f"wg_{kind}{t}", [P, S], F32) for t in range(PACK)] for kind in ("arr", "dep")}
         wa_raw = [[sb(f"wa_raw{c}_{a}", [P, PACK * WA_COLS], F32) for a in range(KP)] for c in range(WA_CHUNKS)]
-        res_t = [sb(f"res{b}", [P, T2], F32) for b in range(RES_BUFS)]
-        pages = {"arr": [], "dep": [sb("page_dep0", [P, T2], F32)]}
+        wa_wide = [sb(f"wa_wide{a}", [P, PACK * PASS], F32) for a in range(KP)]
+        res_t = [sb(f"res{b}", [P, T2], F32) for b in range(RES_RING)]
+        pages = {kind: [sb(f"page_{kind}{b}", [P, T2], F32) for b in range(2)] for kind in ("dep", "arr")}
         ident = sb("ident", [P, P], F32)
-        gain_rows = sb("gain_rows", [P, P], F32)
-        gain_t = sb("gain_t", [P, TILES], F32)
-        warm = sb("warm", [P, 2], F32)
+        gain_t = sb("gain_t", [P, PACK], F32)
+        gain_dealt = sb("gain_dealt", [P, 16], F32)
 
-        def load_scale_rows(queue, dst, src):
+        def dealt(rows, t):
+            return rows.rearrange("(c t i) w -> t c i w", t=PACK, i=PACK)[t]
+
+        def load_wd(g):
+            cols = wd_words.rearrange("a p c -> p a c")[:, :, g * 2 * PASS : (g + 1) * 2 * PASS]
+            nc.sync.dma_start(out=wd_raw[g][:].bitcast(I32), in_=cols.bitcast(I32))
+
+        def load_wa(dst, a, lo, hi):
+            nc.sync.dma_start(
+                out=dst[:].rearrange("p (j c) -> p j c", j=PACK),
+                in_=wa[a * PASS : (a + 1) * PASS, lo:hi].rearrange("(p j) c -> p j c", j=PACK),
+            )
+
+        def load_wg_dealt(kind, t):
             for q in range(4):
-                queue.dma_start(
-                    out=dst[32 * q : 32 * q + 4, :, :].bitcast(I32),
-                    in_=src[:, 4 * q : 4 * q + 4, :].rearrange("a r c -> r a c").bitcast(I32),
-                )
-
-        def load_table(a):
-            nc.sync.dma_start(out=table[a][:], in_=tab_words[a].rearrange("p t i -> p (t i)").bitcast(I32))
-
-        def load_wa(c):
-            for a in range(KP):
-                rows = wa[a * PASS : (a + 1) * PASS, c * WA_COLS : (c + 1) * WA_COLS]
-                nc.sync.dma_start(
-                    out=wa_raw[c][a][:].rearrange("p (j c) -> p j c", j=PACK),
-                    in_=rows.rearrange("(p j) c -> p j c", j=PACK),
-                )
+                nc.sync.dma_start(out=wg_dealt[kind][t][32 * q : 32 * q + 32, :], in_=dealt(wg1 if kind == "arr" else wg2, t))
 
         def load_res(i):
-            nc.sync.dma_start(out=res_t[i % RES_BUFS][:], in_=res[i * P : (i + 1) * P, :])
+            rows = res[i * P : (i + 1) * P, :] if i < PACK else dealt(res[PASS:, :], i - PACK)
+            nc.sync.dma_start(out=res_t[i % RES_RING][:], in_=rows)
 
-        nc.vector.memset(table_sc[:].rearrange("p a c -> p (a c)").bitcast(I32), 0)
-        nc.vector.memset(wd_sc[:].rearrange("p a c -> p (a c)").bitcast(I32), 0)
-        nc.gpsimd.memset(warm[:, 0:1], 0.0)
-        nc.scalar.activation(warm[:, 1:2], warm[:, 0:1], ACT.Silu)
-        nc.gpsimd.memset(gain_rows[:], 0.0)
-        make_identity(nc, ident[:])
-        nc.gpsimd.dma_start(out=gain_rows[0:TILES, :], in_=gain.rearrange("(i p) -> i p", p=P))
-        load_scale_rows(nc.gpsimd, table_sc, tab_scales)
-        load_scale_rows(nc.gpsimd, wd_sc, wd_scales)
-        nc.vector.memset(pages["dep"][0][:], 0.0)
+        nc.gpsimd.memset(table_sc[:].bitcast(I32), 0)
+        nc.gpsimd.dma_start(
+            out=table_sc[0 : KP * SCALE_ROWS, :].bitcast(I32), in_=tab_scales.rearrange("a s t -> s a t").bitcast(I32)
+        )
+        nc.gpsimd.memset(wd_sc[:].rearrange("p a c -> p (a c)").bitcast(I32), 0)
+        nc.gpsimd.memset(v_sc[:].rearrange("p a c -> p (a c)").bitcast(I32), 0)
+        for q in range(4):
+            nc.gpsimd.dma_start(
+                out=wd_sc[32 * q : 32 * q + 4, :, :].bitcast(I32),
+                in_=wd_scales[:, 4 * q : 4 * q + 4, :].rearrange("a r c -> r a c").bitcast(I32),
+            )
 
         nc.sync.dma_start(list_t[:], offs)
         for a in range(KP):
-            load_table(a)
-        wd_view = wd_words.rearrange("a p c -> p a c")
-        nc.sync.dma_start(out=wd_a[0][:].bitcast(I32), in_=wd_view[:, :, : 2 * P].bitcast(I32))
+            nc.sync.dma_start(out=table[a][:], in_=tab_words[a].rearrange("p t i -> p (t i)").bitcast(I32))
+            if a == 0:
+                load_wd(0)
         nc.sync.dma_start(lists["dep"][:], offs3)
         nc.sync.dma_start(out=wg["dep"][:], in_=wg2)
-        nc.sync.dma_start(out=wd_a[1][:].bitcast(I32), in_=wd_view[:, :, 2 * P : 4 * P].bitcast(I32))
-        nc.sync.dma_start(out=wd_b[:].bitcast(I32), in_=wd_view[:, :, WD_FIRST * 2 * P :].bitcast(I32))
-        load_wa(0)
+        for a in range(KP):
+            load_wa(wa_raw[0][a], a, 0, WA_COLS)
+        with nc.allow_non_contiguous_dma(reason="one gain for each row of a tile, on its partition"):
+            nc.sync.dma_start(out=gain_t[:], in_=gain[0:PASS].rearrange("(i p) -> p i", p=P))
         nc.sync.dma_start(lists["arr"][:], offs2)
         nc.sync.dma_start(out=wg["arr"][:], in_=wg1)
-        load_wa(1)
+        for a in range(KP):
+            load_wa(wa_raw[1][a], a, WA_COLS, PASS)
         load_res(0)
         load_res(1)
-        load_wa(2)
         load_res(2)
-        load_wa(3)
-        wo_raw = [sb(f"wo_raw{g}", [P, PACK, N], F32, tag=f"big{g}") for g in range(RP)]
+        load_wd(1)
+        load_res(3)
+        gain_view = gain[PASS:].rearrange("(c x) -> c x", x=16)
+        for i in range(PACK):
+            nc.sync.dma_start(out=gain_dealt[i:P:PACK, 0:GAIN_RUN], in_=gain_view[:, i : i + GAIN_RUN])
+        for a in range(KP):
+            load_wg_dealt("dep", a)
+            load_wa(wa_wide[a], a, PASS, H)
+        load_wg_dealt("dep", KP)
 
-        v_sc = [sb(f"v_sc{a}", [P, S], U8) for a in range(KP)]
-        for a in range(KP):
-            nc.vector.tensor_copy(v_sc[a][:], table_sc[:, a, :].indirect(list_t[:]))
-        v_first = sb("v_first", [P, S], U32)
-        v_rest = sb("v_rest", [P, (KP - 1) * S], U32, tag="table_sc")
-        v_words = [v_first[:]] + [v_rest[:, a * S : (a + 1) * S] for a in range(KP - 1)]
-        for a in range(KP):
-            nc.vector.tensor_copy(v_words[a], table[a][:].bitcast(U32).indirect(list_t[:]))
-        for g in range(RP):
-            nc.sync.dma_start(
-                out=wo_raw[g][:], in_=wo[g * PASS : (g + 1) * PASS, :].rearrange("(p j) n -> p j n", j=PACK)
+        v_words = [sb(f"v_words{a}", [P, S], U32) for a in range(KP)]
+        nc.vector.tensor_copy(picked_sc[:], table_sc[:].indirect(list_t[:]))
+        for q in range(4):
+            nc.gpsimd.dma_start(
+                out=v_sc[32 * q : 32 * q + 4, :, :].bitcast(I32), in_=picked_sc[4 * KP * q : 4 * KP * (q + 1), :].bitcast(I32)
             )
-
-        nc.tensor.transpose(word_banks[0][:, 0:P], gain_rows[:], ident[:])
-        nc.scalar.copy(gain_t[:], word_banks[0][:, 0:TILES])
-
-        h_first = sb("h_first", [P, S], F32)
-        wa_codes = [[sb(f"wa_codes{c}_{a}", [P, WA_COLS], U32) for a in range(KP)] for c in range(WA_CHUNKS)]
-        wa_sc = [[sb(f"wa_sc{c}_{a}", [P, WA_COLS], U8) for a in range(KP)] for c in range(WA_CHUNKS)]
-        held = [sb(f"held{b}", [P, T2], F32) for b in range(HOLD)]
-        z_rows = [[sb(f"z_rows{g}_{hb}", [P, 4, 2, 2 * P], BF16) for hb in range(HALVES)] for g in range(RP)]
-        z_in = [sb(f"z_in{hb}", [P, PACK * BANK], BF16) for hb in range(HALVES)]
-        z_codes = {(1, hb): sb(f"z_codes1_{hb}", [P, BANK], U32) for hb in range(HALVES)}
-        z_sc = [[sb(f"z_sc{g}_{hb}", [P, BANK], U8) for hb in range(HALVES)] for g in range(RP)]
-        wo_codes = [sb(f"wo_codes{g}", [P, N], U32) for g in range(RP)]
-        wo_sc = [sb(f"wo_sc{g}", [P, N], U8) for g in range(RP)]
-
-        def quantize_wa(c):
-            for a in range(KP):
-                nc.scalar.copy(
-                    wa_bf[a].rearrange("p (c i j) -> p c j i", i=4, j=PACK),
-                    wa_raw[c][a][:].rearrange("p (j c i) -> p c j i", i=4, j=PACK),
-                )
-            for a in range(KP):
-                nc.vector.quantize_mx(out=wa_codes[c][a][:].bitcast(E4M3), scales=wa_sc[c][a][:], in_=wa_bf[a])
-
-        def quantize_wo(g):
-            for s in range(2):
-                stage = wa_bf[(2 * g + s) % KP]
-                nc.scalar.copy(
-                    stage.rearrange("p (t m j) -> p m j t", t=2, j=PACK),
-                    wo_raw[g][:].rearrange("p j (m t) -> p m j t", t=PACK)[:, :, :, 2 * s : 2 * s + 2],
-                )
-                cols = slice(2 * s * P, 2 * (s + 1) * P)
-                nc.vector.quantize_mx(out=wo_codes[g][:, cols].bitcast(E4M3), scales=wo_sc[g][:, cols], in_=stage)
+        for a in range(KP):
+            nc.vector.tensor_copy(v_words[a][:], table[a][:].bitcast(U32).indirect(list_t[:]))
+        for page in pages["dep"]:
+            nc.gpsimd.memset(page[:], 0.0)
+        make_identity(nc, ident[:])
+        for page in pages["arr"]:
+            nc.gpsimd.memset(page[:], 0.0)
+        wo_raw = [sb(f"wo_raw{g}", [P, PACK * N], F32, tag=f"big{g}") for g in range(RP)]
+        nc.sync.dma_start(
+            out=wo_raw[0][:].rearrange("p (j n) -> p j n", j=PACK), in_=wo[0:PASS, :].rearrange("(p j) n -> p j n", j=PACK)
+        )
+        for t in range(PACK):
+            load_wg_dealt("arr", t)
+            nc.sync.dma_start(out=wo_raw[1][:, t * N : (t + 1) * N], in_=dealt(wo[PASS:, :], t))
 
         steps = step_order()
+        last = len(steps) - 1
         where = {step: j for j, step in enumerate(steps)}
+        stages = [sb(f"stage{c}", [P, KP * PACK * WA_COLS], BF16) for c in range(WA_CHUNKS)]
+        wa_codes = [sb(f"wa_codes{c}", [P, KP * WA_COLS], U32) for c in range(WA_CHUNKS)]
+        wa_sc = {}
+        wide_codes = sb("wide_codes", [P, KP * PASS], U32)
+        wide_sc = sb("wide_sc", [P, KP * PASS], U8)
+        wd_codes = sb("wd_codes", [P, PACK * KP * 2 * P], U8)
+        wd_sc_dealt = sb("wd_sc_dealt", [P, PACK * KP * P], U8)
+        wo_codes = sb("wo_codes", [P, RP * N], U32)
+        wo_sc = sb("wo_sc", [P, RP * N], U8)
+        z_rows = [sb(f"z_rows{hb}", [P, 4, 2, 2 * P], BF16) for hb in range(HALVES)]
+        z_in = sb("z_in", [P, PACK * T2], BF16)
+        z_codes = [sb(f"z_codes{g}", [P, T2], U32) for g in range(RP)]
+        z_sc = [None, sb("z_sc1", [P, T2], U8)]
 
-        def h_stage(j):
-            return h_first[:] if j == 0 else held[(j - 1) % HOLD][:, 0:S]
+        def cast_wa(c):
+            for a in range(KP):
+                nc.scalar.copy(
+                    stages[c][:, a * PACK * WA_COLS : (a + 1) * PACK * WA_COLS].rearrange("p (c i j) -> p c j i", i=4, j=PACK),
+                    wa_raw[c][a][:].rearrange("p (j c i) -> p c j i", i=4, j=PACK),
+                )
 
-        free_raw = [wa_raw[c][a] for c in range(WA_CHUNKS) for a in (2, 0)] + [wa_raw[c][1] for c in range(WA_CHUNKS)]
-        silu_tiles = {}
+        def quantize_wa(c):
+            wa_sc[c] = sb(f"wa_sc{c}", [P, KP * WA_COLS], U8, tag=f"pin_wa{c}")
+            width = KP * WA_COLS // 2
+            for h in range(2):
+                cols = slice(h * width, (h + 1) * width)
+                nc.vector.quantize_mx(
+                    out=wa_codes[c][:, cols].bitcast(E4M3), scales=wa_sc[c][:, cols],
+                    in_=stages[c][:, PACK * h * width : PACK * (h + 1) * width],
+                )
+
+        def deal_wd():
+            nc.vector.tensor_copy(
+                wd_codes[:].bitcast(I32).rearrange("p (t a c w) -> p a c t w", t=PACK, a=KP, w=2),
+                wd_raw[1][:].bitcast(I32).rearrange("p a (c t w) -> p a c t w", t=PACK, w=2),
+            )
+            nc.vector.tensor_copy(
+                wd_sc_dealt[:].bitcast(I32).rearrange("p (t a c) -> p a c t", t=PACK, a=KP),
+                wd_sc[:, :, PASS:].bitcast(I32).rearrange("p a (c t) -> p a c t", t=PACK),
+            )
+
+        def cast_wide(a):
+            wide_stage = later("wide_stage", [P, KP * PACK * PASS], BF16, "pin_wide")
+            nc.scalar.copy(
+                wide_stage[:, a * PACK * PASS : (a + 1) * PACK * PASS].rearrange("p (t c i j) -> p c t j i", t=PACK, i=PACK, j=PACK),
+                wa_wide[a][:].rearrange("p (j c t i) -> p c t j i", j=PACK, t=PACK, i=PACK),
+            )
+
+        def quantize_wide():
+            for lo, hi in ((0, 2 * PASS), (2 * PASS, KP * PASS)):
+                nc.vector.quantize_mx(
+                    out=wide_codes[:, lo:hi].bitcast(E4M3), scales=wide_sc[:, lo:hi],
+                    in_=made["wide_stage"][:, PACK * lo : PACK * hi],
+                )
+
+        def cast_wo():
+            wo_stage = later("wo_stage", [P, RP * PACK * N], BF16, "pin_wide")
+            for g in range(RP):
+                for s in range(2):
+                    lo = (2 * g + s) * 2 * PACK * P
+                    nc.scalar.copy(
+                        wo_stage[:, lo : lo + 2 * PACK * P].rearrange("p (t m j) -> p m j t", t=2, j=PACK),
+                        wo_raw[g][:].rearrange("p (j m t) -> p m j t", j=PACK, t=PACK)[:, :, :, 2 * s : 2 * s + 2],
+                    )
+
+        def h_tile(j):
+            return later(f"h_step{j}", [P, S], F32, {Z0_STEP: "pin_z", WIDE_STEP - 1: "pin_wide", 0: "pin_wa0", 1: "stage0", 2: "pin_wa1", 4: "stage1"}.get(j, f"h{j % H_RING}"))
+
+        silu_tags = {
+            0: "wa_raw1_0", 1: "wa_raw1_2", 2: "wa_raw0_1", 3: "wa_raw0_0", 4: "wa_raw0_2", 5: "wa_raw1_1",
+            6: "big2", 7: "wd_raw0", 9: "wa_wide2", 12: "big1",
+        }
+        silu_again = {8: 0, 10: 1, 11: 2, 13: 3, 14: 4, 15: 5}
 
         def silu_tile(j):
-            if j not in silu_tiles:
-                if j in WO_STEPS:
-                    silu_tiles[j] = sb(f"silu{j}", [P, T2], F32, tag=f"big{WO_STEPS.index(j)}")
-                else:
-                    silu_tiles[j] = free_raw[j % len(free_raw)]
-            return silu_tiles[j]
+            j = silu_again.get(j, j)
+            return later(f"silu_step{j}", [P, T2], F32, silu_tags[j])
 
-        def gained(j):
-            return silu_tile(j) if j in GAIN_ON_SCALAR else held[j % HOLD]
+        def page_of(j):
+            kind, i = steps[j]
+            return pages[kind][i % 2]
+
+        def gain_col(i):
+            return gain_t[:, i : i + 1] if i < PACK else gain_dealt[:, PACK * (i - PACK) : PACK * (i - PACK) + 1]
+
+        def z_plane(i):
+            return later("z_planes", [P, PACK * T2], BF16, "wa_wide0")[:, (i - PACK) * T2 : (i - PACK + 1) * T2]
 
         def product(j):
             kind, i = steps[j]
-            bank = h_banks[j % 2]
+            bank = (h_banks + word_banks)[j % 4] if j < WIDE_RING else h_banks[j % 2]
             for a in range(KP):
-                if kind == "arr":
+                t = i - PACK
+                if kind == "arr" and i < PACK:
                     c, col = divmod(i * P, WA_COLS)
-                    lhs = wa_codes[c][a][:, col : col + P].bitcast(E4M3)
-                    lhs_sc = wa_sc[c][a][:, col : col + P]
-                else:
-                    src, n = (wd_a[i], 0) if i < WD_FIRST else (wd_b, i - WD_FIRST)
-                    lhs = src[:, a, n * 2 * P : (n + 1) * 2 * P].bitcast(E2M1)
+                    cols = slice(a * WA_COLS + col, a * WA_COLS + col + P)
+                    lhs, lhs_sc = wa_codes[c][:, cols].bitcast(E4M3), wa_sc[c][:, cols]
+                elif kind == "arr":
+                    cols = slice(a * PASS + t * P, a * PASS + (t + 1) * P)
+                    lhs, lhs_sc = wide_codes[:, cols].bitcast(E4M3), wide_sc[:, cols]
+                elif i < PACK:
+                    lhs = wd_raw[0][:, a, i * 2 * P : (i + 1) * 2 * P].bitcast(E2M1)
                     lhs_sc = wd_sc[:, a, i * P : (i + 1) * P]
+                else:
+                    n = t * KP + a
+                    lhs, lhs_sc = wd_codes[:, n * 2 * P : (n + 1) * 2 * P].bitcast(E2M1), wd_sc_dealt[:, n * P : (n + 1) * P]
                 nc.tensor.matmul_mx(
-                    out=bank[:], lhsT=lhs, lhsT_scale=lhs_sc, rhs=v_words[a].bitcast(E4M3),
-                    rhs_scale=v_sc[a][:], start=(a == 0), stop=(a == KP - 1),
+                    out=bank[:], lhsT=lhs, lhsT_scale=lhs_sc, rhs=v_words[a][:].bitcast(E4M3),
+                    rhs_scale=v_sc[:, a, :], start=(a == 0), stop=(a == KP - 1),
                 )
-            nc.scalar.copy(h_stage(j), bank[:])
+            if j < WEIGHED_FIRST:
+                nc.vector.tensor_tensor(h_tile(j)[:], bank[:], wg[kind][:], MULT)
+            else:
+                nc.scalar.copy(h_tile(j)[:], bank[:])
 
         def scatter(j):
             kind, i = steps[j]
-            page = pages[kind][i % 2]
-            nc.vector.tensor_tensor(page[:].indirect(lists[kind][:]), h_stage(j), wg[kind][:], MULT)
+            window = page_of(j)[:].indirect(lists[kind][:])
+            if j < WEIGHED_FIRST:
+                nc.vector.tensor_copy(window, h_tile(j)[:])
+            else:
+                nc.vector.tensor_tensor(window, h_tile(j)[:], (wg[kind] if i < PACK else wg_dealt[kind][i - PACK])[:], MULT)
+
+        halves = [slice(hb * BANK, (hb + 1) * BANK) for hb in range(HALVES)]
 
         def activate(j):
             kind, i = steps[j]
-            s_tile = silu_tile(j)
-            split = j in GAIN_ON_SCALAR or j == len(steps) - 1
-            parts = [slice(hb * BANK, (hb + 1) * BANK) for hb in range(HALVES)] if split else [slice(0, T2)]
-            for cols in parts:
-                nc.scalar.activation(s_tile[:, cols], pages[kind][i % 2][:, cols], ACT.Silu)
-            for cols in parts:
-                dst = gained(j)[:, cols]
-                if j in GAIN_ON_SCALAR:
-                    nc.scalar.activation(dst, s_tile[:, cols], ACT.Copy, scale=gain_t[:, i : i + 1])
-                else:
-                    nc.vector.tensor_scalar(dst, s_tile[:, cols], gain_t[:, i : i + 1], None, MULT)
+            tile = silu_tile(j)
+            if kind == "dep" or i >= PACK:
+                nc.scalar.activation(tile[:], page_of(j)[:], ACT.Silu)
+                return
+            for cols in halves:
+                nc.scalar.activation(tile[:, cols], page_of(j)[:, cols], ACT.Silu)
+            for cols in halves:
+                nc.scalar.activation(tile[:, cols], tile[:, cols], ACT.Copy, scale=gain_col(i))
 
-        def add_term(i, hb, src, first, last):
+        def combine(j):
+            kind, i = steps[j]
+            tile = silu_tile(j)
+            if kind == "dep":
+                nc.vector.scalar_tensor_tensor(tile[:], tile[:], gain_col(i), res_t[i % RES_RING][:], MULT, ADD)
+                if i + RES_RING < TILES:
+                    load_res(i + RES_RING)
+            elif i >= PACK:
+                nc.vector.scalar_tensor_tensor(z_plane(i), tile[:], gain_col(i), silu_tile(where[("dep", i)])[:], MULT, ADD)
+
+        def add_term(i, hb, kind):
             bank = sum_banks[2 * (i % 2) + hb]
+            src = silu_tile(where[(kind, i)])
             for b in range(4):
                 m0 = (4 * hb + b) * P
                 nc.tensor.matmul(
                     bank[:, b * P : (b + 1) * P], src[:, m0 : m0 + P], ident[:],
-                    start=(first and b == 0), stop=(last and b == 3), is_transpose=True,
+                    start=(kind == "dep" and b == 0), stop=(kind == "arr" and b == 3), is_transpose=True,
                 )
 
-        def open_sum(i):
-            early = min(where[("arr", i)], where[("dep", i)])
-            for hb in range(HALVES):
-                add_term(i, hb, res_t[i % RES_BUFS], True, False)
-                add_term(i, hb, gained(early), False, False)
-            if i + RES_BUFS < TILES:
-                load_res(i + RES_BUFS)
-
-        def close_sum(i, hb):
-            late = max(where[("arr", i)], where[("dep", i)])
-            add_term(i, hb, gained(late), False, True)
-            g, quarter = divmod(i, 4)
+        def round_sum(i, hb):
             nc.scalar.copy(
-                z_rows[g][hb][:, :, :, 64 * quarter : 64 * (quarter + 1)].rearrange("p b u (q e) -> p b u q e", e=2),
+                z_rows[hb][:, :, :, 64 * i : 64 * (i + 1)].rearrange("p b u (q e) -> p b u q e", e=2),
                 sum_banks[2 * (i % 2) + hb][:].rearrange("p (b q u e) -> p b u q e", b=4, u=2, e=2),
             )
 
-        def interleave_z(g, q, bank, copy):
+        def interleave_z(q, bank):
             hb, pair = divmod(q, 2)
-            words = z_rows[g][hb][:].bitcast(F32)
+            words = z_rows[hb][:].bitcast(F32)
             for b in range(2):
                 for u in range(2):
                     col = (2 * b + u) * P
                     nc.tensor.transpose(bank[:, col : col + P], words[:, 2 * pair + b, u, :], ident[:])
-            copy(
-                z_in[hb][:].bitcast(F32)[:, pair * BANK : (pair + 1) * BANK].rearrange("p (b m u) -> p b m u", b=2, u=2),
+            nc.scalar.copy(
+                z_in[:].bitcast(F32)[:, q * BANK : (q + 1) * BANK].rearrange("p (b m u) -> p b m u", b=2, u=2),
                 bank[:].rearrange("p (b u m) -> p b m u", b=2, u=2),
             )
 
-        def quantize_z(g, hb, lo, hi):
-            nc.vector.quantize_mx(
-                out=z_codes[(g, hb)][:, lo:hi].bitcast(E4M3), scales=z_sc[g][hb][:, lo:hi],
-                in_=z_in[hb][:, PACK * lo : PACK * hi],
+        def weave(copy, lo, hi, t0, t1):
+            c0, c1 = lo // PACK, hi // PACK
+            copy(
+                z_in[:].rearrange("p (c i t) -> p c t i", i=PACK, t=PACK)[:, c0:c1, t0:t1, :],
+                made["z_planes"][:].rearrange("p (t c i) -> p c t i", i=PACK, t=PACK)[:, c0:c1, t0:t1, :],
             )
 
-        y_banks = [banks[0:2], banks[6:8], banks[2:4], banks[4:6]]
+        def quantize_z(g, lo, hi):
+            nc.vector.quantize_mx(
+                out=z_codes[g][:, lo:hi].bitcast(E4M3), scales=z_sc[g][:, lo:hi], in_=z_in[:, PACK * lo : PACK * hi]
+            )
+
+        y_banks = [banks[2:4], banks[4:6], banks[6:8], banks[0:2]]
 
         def y_pass(g, q):
-            hb, pair = divmod(q, 2)
-            cols = slice(pair * QUART, (pair + 1) * QUART)
+            cols = slice(q * QUART, (q + 1) * QUART)
             for t in range(PACK):
+                w = slice(g * N + t * P, g * N + (t + 1) * P)
                 nc.tensor.matmul_mx(
                     out=y_banks[q][t // 2][:, (t % 2) * QUART : (t % 2 + 1) * QUART],
-                    lhsT=wo_codes[g][:, t * P : (t + 1) * P].bitcast(E4M3),
-                    lhsT_scale=wo_sc[g][:, t * P : (t + 1) * P], rhs=z_codes[(g, hb)][:, cols].bitcast(E4M3),
-                    rhs_scale=z_sc[g][hb][:, cols], start=(g == 0 and t % 2 == 0), stop=(g == RP - 1 and t % 2 == 1),
+                    lhsT=wo_codes[:, w].bitcast(E4M3), lhsT_scale=wo_sc[:, w],
+                    rhs=z_codes[g][:, cols].bitcast(E4M3), rhs_scale=z_sc[g][:, cols],
+                    start=(g == 0 and t % 2 == 0), stop=(g == RP - 1 and t % 2 == 1),
                 )
 
-        last = len(steps) - 1
-        closes = {max(where[("arr", i)], where[("dep", i)]): i for i in range(TILES)}
-        def finish_sum(j):
-            if j in closes:
-                for hb in range(HALVES):
-                    close_sum(closes[j], hb)
-                if closes[j] == 3:
-                    for q in range(4):
-                        interleave_z(0, q, word_banks[q % 2], nc.scalar.copy)
+        def finish_sum(i):
+            for hb in range(HALVES):
+                add_term(i, hb, "dep")
+                add_term(i, hb, "arr")
+                round_sum(i, hb)
+            if i == PACK - 1:
+                for q in range(CHUNKS):
+                    interleave_z(q, word_banks[q % 2])
 
+        issued = [1]
+        casts = (lambda: cast_wa(1), cast_wo)
+        quantizers = (
+            lambda: quantize_wa(0), lambda: quantize_wa(1), quantize_wide,
+            lambda: nc.vector.quantize_mx(out=wo_codes[:].bitcast(E4M3), scales=wo_sc[:], in_=made["wo_stage"][:]),
+        )
+        cast_wa(0)
         product(0)
-        stage_all = sb("stage_all", [P, KP * PACK * WA_COLS], BF16, tag="wd_a0")
-        wa_bf = [stage_all[:, a * PACK * WA_COLS : (a + 1) * PACK * WA_COLS] for a in range(KP)]
-        product(1)
-        scatter(0)
-        for kind, tag in (("dep", "big2"), ("arr", "wd_a1"), ("arr", "h_first")):
-            page = sb("page_" + tag, [P, T2], F32, tag=tag)
-            nc.gpsimd.memset(page[:], 0.0)
-            pages[kind].append(page)
         for j in range(last):
-            if j % 2 == 0 and j // 2 < WA_CHUNKS:
-                quantize_wa(j // 2)
-            if j in WO_STEPS:
-                quantize_wo(WO_STEPS.index(j))
-            if j + 2 <= last:
-                product(j + 2)
-            scatter(j + 1)
-            if j + 1 in Z0_STEPS:
-                hb = Z0_STEPS.index(j + 1)
-                z_codes[(0, hb)] = sb(f"z_codes0_{hb}", [P, BANK], U32, tag=("wg_dep" if j + 1 == last else f"held{j % HOLD}"))
-                quantize_z(0, hb, 0, BANK)
+            scatter(j)
+            if j in QUANTIZE_STEPS:
+                quantizers[QUANTIZE_STEPS.index(j)]()
+            if j == Z0_STEP:
+                z_sc[0] = sb("z_sc0", [P, T2], U8, tag="pin_z")
+                quantize_z(0, 0, T2)
+            if j == DEAL_STEP:
+                deal_wd()
+            if j > 0:
+                combine(j - 1)
+            for ahead in range(issued[0], min(j + AHEAD, last) + 1):
+                if j < NEEDS.get(ahead, 0):
+                    break
+                product(ahead)
+                issued[0] = ahead + 1
+            if j in CAST_STEPS:
+                casts[CAST_STEPS.index(j)]()
+            if j == last - 1:
+                weave(nc.scalar.copy, 0, T2, 0, 2)
             activate(j)
-            finish_sum(j - SUM_LAG)
-            if j in closes:
-                open_sum(closes[j])
+            if WIDE_STEP <= j < WIDE_STEP + KP:
+                cast_wide(j - WIDE_STEP)
+            if j > 0 and steps[j - 1][0] == "arr" and steps[j - 1][1] < PACK:
+                finish_sum(steps[j - 1][1])
+            if j == QUANTIZE_STEPS[-1]:
+                for q in range(CHUNKS):
+                    y_pass(0, q)
 
-        for j in range(last - SUM_LAG, last):
-            finish_sum(j)
-        open_sum(TILES - 1)
-        y_pass(0, 0)
-        y_pass(0, 1)
-        activate(last)
-        for hb in range(HALVES):
-            close_sum(TILES - 1, hb)
-        tail_banks = banks[2:6]
-        for q in range(4):
-            interleave_z(1, q, tail_banks[q], nc.vector.tensor_copy if q % 2 == 0 else nc.scalar.copy)
+        scatter(last)
+        combine(last - 1)
+        i = TILES - 1
+        mine, other = silu_tile(last), silu_tile(where[("dep", i)])
+        quarters = [slice(q * QUART, (q + 1) * QUART) for q in range(CHUNKS)]
+        for cols in quarters:
+            nc.scalar.activation(mine[:, cols], page_of(last)[:, cols], ACT.Silu)
+        for q, cols in enumerate(quarters):
+            nc.vector.scalar_tensor_tensor(z_plane(i)[:, cols], mine[:, cols], gain_col(i), other[:, cols], MULT, ADD)
+            weave(nc.vector.tensor_copy, q * QUART, (q + 1) * QUART, 2, PACK)
+            quantize_z(1, q * QUART, (q + 1) * QUART)
+            y_pass(1, q)
         y_view = out_0.rearrange("(p t) m -> p t m", t=PACK)
         codes_view = out_1[0].rearrange("p m t -> p (m t)").bitcast(I32)
         y_sc = sb("y_sc", [P, T2], U8)
-        y_codes = [sb(f"y_codes{q}", [P, QUART], U32) for q in range(4)]
-        for q in range(4):
-            quantize_z(1, q // 2, (q % 2) * QUART, (q % 2 + 1) * QUART)
-            if q >= 2:
-                y_pass(0, q)
-            y_pass(1, q)
-        for q in range(4):
+        y_codes = [sb(f"y_codes{q}", [P, QUART], U32) for q in range(CHUNKS)]
+        y_sb = [sb(f"y_sb{h}", [P, 2 * PACK * QUART], F32, tag=("wa_wide1", "big0")[h]) for h in range(2)]
+        for q in range(CHUNKS):
             cols = slice(q * QUART, (q + 1) * QUART)
-            y_sb = wa_raw[q][1]
-            y_bf = z_rows[0][q // 2][:].rearrange("p b u w -> p (b u w)")[:, (q % 2) * PACK * QUART : (q % 2 + 1) * PACK * QUART]
+            rows = y_sb[q // 2][:, (q % 2) * PACK * QUART : (q % 2 + 1) * PACK * QUART]
+            rounded = z_rows[q // 2][:].rearrange("p b u w -> p (b u w)")[:, (q % 2) * PACK * QUART : (q % 2 + 1) * PACK * QUART]
             for s in range(2):
-                half = y_sb[:, s * BANK : (s + 1) * BANK]
-                nc.scalar.copy(half, y_banks[q][s][:])
-                nc.sync.dma_start(out=y_view[:, 2 * s : 2 * s + 2, cols], in_=half.rearrange("p (t m) -> p t m", t=2))
+                nc.scalar.copy(rows[:, s * BANK : (s + 1) * BANK], y_banks[q][s][:])
+            nc.sync.dma_start(out=y_view[:, :, cols], in_=rows.rearrange("p (t m) -> p t m", t=PACK))
             nc.vector.tensor_copy(
-                y_bf.rearrange("p (c i t) -> p c t i", i=4, t=PACK),
-                y_sb[:].rearrange("p (t c i) -> p c t i", i=4, t=PACK),
+                rounded.rearrange("p (c i t) -> p c t i", i=PACK, t=PACK),
+                rows.rearrange("p (t c i) -> p c t i", i=PACK, t=PACK),
             )
-            nc.vector.quantize_mx(out=y_codes[q][:].bitcast(E4M3), scales=y_sc[:, cols], in_=y_bf)
+            nc.vector.quantize_mx(out=y_codes[q][:].bitcast(E4M3), scales=y_sc[:, cols], in_=rounded)
             nc.sync.dma_start(out=codes_view[:, cols], in_=y_codes[q][:].bitcast(I32))
         for q in range(4):
             queue = nc.sync if q % 2 == 0 else nc.scalar

@@ -30,10 +30,10 @@ QUART = 256
 CHUNKS = T2 // QUART
 WA_COLS = 256
 WA_CHUNKS = PASS // WA_COLS
-SCALE_ROWS = 16
 RES_RING = 4
 H_RING = 3
 AHEAD = 2
+RES_BY_TRANSPOSE = 2
 WIDE_RING = 8
 GAIN_RUN = 13
 CAST_STEPS = (0, 11)
@@ -75,9 +75,7 @@ def tile_list_parish_migration_pages_kernel(
         list_t = sb("list_t", [P, S // 16], U16)
         lists = {"arr": sb("list_a", [P, S // 16], U16), "dep": sb("list_d", [P, S // 16], U16)}
         table = [sb(f"table{a}", [P, T], I32, tag=f"big{a}") for a in range(KP)]
-        table_sc = sb("table_sc", [P, T], U8)
-        picked_sc = sb("picked_sc", [P, S], U8)
-        v_sc = sb("v_sc", [P, KP, S], U8)
+        table_sc = sb("table_sc", [P, KP, T], U8)
         wd_sc = sb("wd_sc", [P, KP, H], U8)
         wd_raw = [sb(f"wd_raw{g}", [P, KP, 2 * PASS], U8) for g in range(RP)]
         wg = {kind: sb("wg_" + kind, [P, S], F32) for kind in ("arr", "dep")}
@@ -111,30 +109,40 @@ def tile_list_parish_migration_pages_kernel(
             rows = res[i * P : (i + 1) * P, :] if i < PACK else dealt(res[PASS:, :], i - PACK)
             nc.sync.dma_start(out=res_t[i % RES_RING][:], in_=rows)
 
-        nc.gpsimd.memset(table_sc[:].bitcast(I32), 0)
-        nc.gpsimd.dma_start(
-            out=table_sc[0 : KP * SCALE_ROWS, :].bitcast(I32), in_=tab_scales.rearrange("a s t -> s a t").bitcast(I32)
-        )
-        nc.gpsimd.memset(wd_sc[:].rearrange("p a c -> p (a c)").bitcast(I32), 0)
-        nc.gpsimd.memset(v_sc[:].rearrange("p a c -> p (a c)").bitcast(I32), 0)
-        for q in range(4):
-            nc.gpsimd.dma_start(
-                out=wd_sc[32 * q : 32 * q + 4, :, :].bitcast(I32),
-                in_=wd_scales[:, 4 * q : 4 * q + 4, :].rearrange("a r c -> r a c").bitcast(I32),
-            )
-
-        nc.sync.dma_start(list_t[:], offs)
-        for a in range(KP):
+        def load_table(a):
             nc.sync.dma_start(out=table[a][:], in_=tab_words[a].rearrange("p t i -> p (t i)").bitcast(I32))
-            if a == 0:
-                load_wd(0)
+
+        def load_scale_rows(dst, src):
+            rows = src.rearrange("a (q r) c -> r q a c", r=4)
+            for r in range(4):
+                nc.scalar.dma_start(out=dst[r:P:32, :, :].bitcast(I32), in_=rows[r].bitcast(I32))
+
+        gain_view = gain[PASS:].rearrange("(c x) -> c x", x=16)
+
+        def load_gain_dealt(i):
+            nc.sync.dma_start(out=gain_dealt[i:P:PACK, 0:GAIN_RUN], in_=gain_view[:, i : i + GAIN_RUN])
+
+        sc_words = table_sc[:].rearrange("p a c -> p (a c)").bitcast(I32)
+        half_words = KP * T // 8
+        nc.vector.memset(sc_words[:, :half_words], 0)
+        nc.gpsimd.memset(sc_words[:, half_words:], 0)
+        nc.gpsimd.memset(wd_sc[:].rearrange("p a c -> p (a c)").bitcast(I32), 0)
+        nc.sync.dma_start(list_t[:], offs)
         nc.sync.dma_start(lists["dep"][:], offs3)
+        nc.sync.dma_start(lists["arr"][:], offs2)
+        with nc.allow_non_contiguous_dma(reason="one gain for each row of a tile, on its partition"):
+            nc.sync.dma_start(out=gain_t[:], in_=gain[0:PASS].rearrange("(i p) -> p i", p=P))
+        load_gain_dealt(0)
+        load_gain_dealt(1)
+        load_table(0)
+        load_table(1)
+        load_scale_rows(table_sc, tab_scales)
+        load_wd(0)
+        load_table(2)
+        load_scale_rows(wd_sc, wd_scales)
         nc.sync.dma_start(out=wg["dep"][:], in_=wg2)
         for a in range(KP):
             load_wa(wa_raw[0][a], a, 0, WA_COLS)
-        with nc.allow_non_contiguous_dma(reason="one gain for each row of a tile, on its partition"):
-            nc.sync.dma_start(out=gain_t[:], in_=gain[0:PASS].rearrange("(i p) -> p i", p=P))
-        nc.sync.dma_start(lists["arr"][:], offs2)
         nc.sync.dma_start(out=wg["arr"][:], in_=wg1)
         for a in range(KP):
             load_wa(wa_raw[1][a], a, WA_COLS, PASS)
@@ -143,22 +151,22 @@ def tile_list_parish_migration_pages_kernel(
         load_res(2)
         load_wd(1)
         load_res(3)
-        gain_view = gain[PASS:].rearrange("(c x) -> c x", x=16)
-        for i in range(PACK):
-            nc.sync.dma_start(out=gain_dealt[i:P:PACK, 0:GAIN_RUN], in_=gain_view[:, i : i + GAIN_RUN])
+        load_gain_dealt(2)
+        load_gain_dealt(3)
         for a in range(KP):
             load_wg_dealt("dep", a)
             load_wa(wa_wide[a], a, PASS, H)
         load_wg_dealt("dep", KP)
 
-        v_words = [sb(f"v_words{a}", [P, S], U32) for a in range(KP)]
-        nc.vector.tensor_copy(picked_sc[:], table_sc[:].indirect(list_t[:]))
-        for q in range(4):
-            nc.gpsimd.dma_start(
-                out=v_sc[32 * q : 32 * q + 4, :, :].bitcast(I32), in_=picked_sc[4 * KP * q : 4 * KP * (q + 1), :].bitcast(I32)
-            )
+        v_sc = sb("v_sc", [P, KP, S], U8)
+        v_first = sb("v_first", [P, S], U32)
+        nc.vector.tensor_copy(v_first[:], table[0][:].bitcast(U32).indirect(list_t[:]))
         for a in range(KP):
-            nc.vector.tensor_copy(v_words[a][:], table[a][:].bitcast(U32).indirect(list_t[:]))
+            nc.vector.tensor_copy(v_sc[:, a, :], table_sc[:, a, :].indirect(list_t[:]))
+        v_rest = sb("v_rest", [P, (KP - 1) * S], U32, tag="table_sc")
+        v_words = [v_first[:]] + [v_rest[:, a * S : (a + 1) * S] for a in range(KP - 1)]
+        for a in range(1, KP):
+            nc.vector.tensor_copy(v_words[a], table[a][:].bitcast(U32).indirect(list_t[:]))
         for page in pages["dep"]:
             nc.gpsimd.memset(page[:], 0.0)
         make_identity(nc, ident[:])
@@ -180,8 +188,6 @@ def tile_list_parish_migration_pages_kernel(
         wa_sc = {}
         wide_codes = sb("wide_codes", [P, KP * PASS], U32)
         wide_sc = sb("wide_sc", [P, KP * PASS], U8)
-        wd_codes = sb("wd_codes", [P, PACK * KP * 2 * P], U8)
-        wd_sc_dealt = sb("wd_sc_dealt", [P, PACK * KP * P], U8)
         wo_codes = sb("wo_codes", [P, RP * N], U32)
         wo_sc = sb("wo_sc", [P, RP * N], U8)
         z_rows = [sb(f"z_rows{hb}", [P, 4, 2, 2 * P], BF16) for hb in range(HALVES)]
@@ -207,6 +213,8 @@ def tile_list_parish_migration_pages_kernel(
                 )
 
         def deal_wd():
+            wd_codes = later("wd_codes", [P, PACK * KP * 2 * P], U8, "stage1")
+            wd_sc_dealt = later("wd_sc_dealt", [P, PACK * KP * P], U8, "stage0")
             nc.vector.tensor_copy(
                 wd_codes[:].bitcast(I32).rearrange("p (t a c w) -> p a c t w", t=PACK, a=KP, w=2),
                 wd_raw[1][:].bitcast(I32).rearrange("p a (c t w) -> p a c t w", t=PACK, w=2),
@@ -280,9 +288,10 @@ def tile_list_parish_migration_pages_kernel(
                     lhs_sc = wd_sc[:, a, i * P : (i + 1) * P]
                 else:
                     n = t * KP + a
-                    lhs, lhs_sc = wd_codes[:, n * 2 * P : (n + 1) * 2 * P].bitcast(E2M1), wd_sc_dealt[:, n * P : (n + 1) * P]
+                    lhs = made["wd_codes"][:, n * 2 * P : (n + 1) * 2 * P].bitcast(E2M1)
+                    lhs_sc = made["wd_sc_dealt"][:, n * P : (n + 1) * P]
                 nc.tensor.matmul_mx(
-                    out=bank[:], lhsT=lhs, lhsT_scale=lhs_sc, rhs=v_words[a][:].bitcast(E4M3),
+                    out=bank[:], lhsT=lhs, lhsT_scale=lhs_sc, rhs=v_words[a].bitcast(E4M3),
                     rhs_scale=v_sc[:, a, :], start=(a == 0), stop=(a == KP - 1),
                 )
             if j < WEIGHED_FIRST:
@@ -303,7 +312,7 @@ def tile_list_parish_migration_pages_kernel(
         def activate(j):
             kind, i = steps[j]
             tile = silu_tile(j)
-            if kind == "dep" or i >= PACK:
+            if i >= (RES_BY_TRANSPOSE if kind == "dep" else PACK):
                 nc.scalar.activation(tile[:], page_of(j)[:], ACT.Silu)
                 return
             for cols in halves:
@@ -314,21 +323,20 @@ def tile_list_parish_migration_pages_kernel(
         def combine(j):
             kind, i = steps[j]
             tile = silu_tile(j)
-            if kind == "dep":
+            if kind == "dep" and i >= RES_BY_TRANSPOSE:
                 nc.vector.scalar_tensor_tensor(tile[:], tile[:], gain_col(i), res_t[i % RES_RING][:], MULT, ADD)
                 if i + RES_RING < TILES:
                     load_res(i + RES_RING)
-            elif i >= PACK:
+            elif kind == "arr" and i >= PACK:
                 nc.vector.scalar_tensor_tensor(z_plane(i), tile[:], gain_col(i), silu_tile(where[("dep", i)])[:], MULT, ADD)
 
-        def add_term(i, hb, kind):
+        def add_term(i, hb, src, first, final):
             bank = sum_banks[2 * (i % 2) + hb]
-            src = silu_tile(where[(kind, i)])
             for b in range(4):
                 m0 = (4 * hb + b) * P
                 nc.tensor.matmul(
                     bank[:, b * P : (b + 1) * P], src[:, m0 : m0 + P], ident[:],
-                    start=(kind == "dep" and b == 0), stop=(kind == "arr" and b == 3), is_transpose=True,
+                    start=(first and b == 0), stop=(final and b == 3), is_transpose=True,
                 )
 
         def round_sum(i, hb):
@@ -375,10 +383,15 @@ def tile_list_parish_migration_pages_kernel(
                 )
 
         def finish_sum(i):
+            terms = [silu_tile(where[(kind, i)]) for kind in ("dep", "arr")]
+            if i < RES_BY_TRANSPOSE:
+                terms = [res_t[i]] + terms
             for hb in range(HALVES):
-                add_term(i, hb, "dep")
-                add_term(i, hb, "arr")
+                for n, src in enumerate(terms):
+                    add_term(i, hb, src, n == 0, n == len(terms) - 1)
                 round_sum(i, hb)
+            if i < RES_BY_TRANSPOSE:
+                load_res(i + RES_RING)
             if i == PACK - 1:
                 for q in range(CHUNKS):
                     interleave_z(q, word_banks[q % 2])

@@ -33,21 +33,25 @@ WA_CHUNKS = PASS // WA_COLS
 RES_RING = 4
 H_RING = 3
 AHEAD = 2
-RES_BY_TRANSPOSE = 2
+OPEN_STEPS = (2, 3, 6, 7, 10, 11)
+TIGHT_FROM = 9
+SUM_STEPS = (4, 5, 8, 9, 12, 13)
+GAIN_ON_VECTOR = (4, 5, 6, 7, 8, 9)
+SUMMED = 6
 WIDE_RING = 8
 GAIN_RUN = 13
-CAST_STEPS = (0, 11)
+CAST_STEPS = (0, 8)
 WIDE_STEP = 4
-NEEDS = {1: 0, 4: 2, 8: 4, 12: 10}
+NEEDS = {1: 0, 4: 2, 8: 4, 11: 9}
 WEIGHED_FIRST = 2
-QUANTIZE_STEPS = (0, 2, 10, 13)
+QUANTIZE_STEPS = (0, 2, 9, 11)
 Z0_STEP = 11
 DEAL_STEP = 4
 
 
 def step_order():
     steps = [(kind, 2 * c + h) for c in range(WA_CHUNKS) for kind in ("dep", "arr") for h in range(2)]
-    return steps + [(kind, i) for kind in ("dep", "arr") for i in range(PACK, TILES)]
+    return steps + [("dep", 4), ("dep", 5), ("dep", 6), ("arr", 4), ("arr", 5), ("dep", 7), ("arr", 6), ("arr", 7)]
 
 
 def tile_list_parish_migration_pages_kernel(
@@ -102,12 +106,12 @@ def tile_list_parish_migration_pages_kernel(
             )
 
         def load_wg_dealt(kind, t):
-            for q in range(4):
+            for q in (0, 2, 1, 3):
                 nc.sync.dma_start(out=wg_dealt[kind][t][32 * q : 32 * q + 32, :], in_=dealt(wg1 if kind == "arr" else wg2, t))
 
         def load_res(i):
             rows = res[i * P : (i + 1) * P, :] if i < PACK else dealt(res[PASS:, :], i - PACK)
-            nc.sync.dma_start(out=res_t[i % RES_RING][:], in_=rows)
+            nc.sync.dma_start(out=res_t[i][:], in_=rows)
 
         def load_table(a):
             nc.sync.dma_start(out=table[a][:], in_=tab_words[a].rearrange("p t i -> p (t i)").bitcast(I32))
@@ -148,15 +152,13 @@ def tile_list_parish_migration_pages_kernel(
             load_wa(wa_raw[1][a], a, WA_COLS, PASS)
         load_res(0)
         load_res(1)
-        load_res(2)
         load_wd(1)
-        load_res(3)
+        for a in range(KP):
+            load_wa(wa_wide[a], a, PASS, H)
+            if a > 0:
+                load_res(1 + a)
         load_gain_dealt(2)
         load_gain_dealt(3)
-        for a in range(KP):
-            load_wg_dealt("dep", a)
-            load_wa(wa_wide[a], a, PASS, H)
-        load_wg_dealt("dep", KP)
 
         v_sc = sb("v_sc", [P, KP, S], U8)
         v_first = sb("v_first", [P, S], U32)
@@ -176,9 +178,15 @@ def tile_list_parish_migration_pages_kernel(
         nc.sync.dma_start(
             out=wo_raw[0][:].rearrange("p (j n) -> p j n", j=PACK), in_=wo[0:PASS, :].rearrange("(p j) n -> p j n", j=PACK)
         )
+        load_wg_dealt("dep", 0)
         for t in range(PACK):
-            load_wg_dealt("arr", t)
             nc.sync.dma_start(out=wo_raw[1][:, t * N : (t + 1) * N], in_=dealt(wo[PASS:, :], t))
+        dealt_steps = [step for step in step_order() if step[1] >= PACK]
+        for n, (kind, i) in enumerate(dealt_steps[1:]):
+            load_wg_dealt(kind, i - PACK)
+            if n < TILES - RES_RING:
+                res_t.append(sb(f"res{RES_RING + n}", [P, T2], F32, tag=f"res{n}"))
+                load_res(RES_RING + n)
 
         steps = step_order()
         last = len(steps) - 1
@@ -239,7 +247,7 @@ def tile_list_parish_migration_pages_kernel(
                 )
 
         def cast_wo():
-            wo_stage = later("wo_stage", [P, RP * PACK * N], BF16, "pin_wide")
+            wo_stage = later("wo_stage", [P, RP * PACK * N], BF16, "wa_wide0")
             for g in range(RP):
                 for s in range(2):
                     lo = (2 * g + s) * 2 * PACK * P
@@ -252,10 +260,10 @@ def tile_list_parish_migration_pages_kernel(
             return later(f"h_step{j}", [P, S], F32, {Z0_STEP: "pin_z", WIDE_STEP - 1: "pin_wide", 0: "pin_wa0", 1: "stage0", 2: "pin_wa1", 4: "stage1"}.get(j, f"h{j % H_RING}"))
 
         silu_tags = {
-            0: "wa_raw1_0", 1: "wa_raw1_2", 2: "wa_raw0_1", 3: "wa_raw0_0", 4: "wa_raw0_2", 5: "wa_raw1_1",
-            6: "big2", 7: "wd_raw0", 9: "wa_wide2", 12: "big1",
+            0: "wa_raw0_2", 1: "wa_raw1_2", 2: "wa_raw0_1", 3: "wa_raw0_0", 4: "wa_raw1_0", 5: "wa_raw1_1",
+            6: "big2", 7: "wd_raw0", 8: "wa_wide2", 9: "big1", 15: "wa_wide1",
         }
-        silu_again = {8: 0, 10: 1, 11: 2, 13: 3, 14: 4, 15: 5}
+        silu_again = {11: 0, 10: 1, 12: 2, 13: 3, 14: 4}
 
         def silu_tile(j):
             j = silu_again.get(j, j)
@@ -312,7 +320,7 @@ def tile_list_parish_migration_pages_kernel(
         def activate(j):
             kind, i = steps[j]
             tile = silu_tile(j)
-            if i >= (RES_BY_TRANSPOSE if kind == "dep" else PACK):
+            if i >= SUMMED or j in GAIN_ON_VECTOR:
                 nc.scalar.activation(tile[:], page_of(j)[:], ACT.Silu)
                 return
             for cols in halves:
@@ -323,11 +331,11 @@ def tile_list_parish_migration_pages_kernel(
         def combine(j):
             kind, i = steps[j]
             tile = silu_tile(j)
-            if kind == "dep" and i >= RES_BY_TRANSPOSE:
-                nc.vector.scalar_tensor_tensor(tile[:], tile[:], gain_col(i), res_t[i % RES_RING][:], MULT, ADD)
-                if i + RES_RING < TILES:
-                    load_res(i + RES_RING)
-            elif kind == "arr" and i >= PACK:
+            if j in GAIN_ON_VECTOR:
+                nc.vector.tensor_scalar(tile[:], tile[:], gain_col(i), None, MULT)
+            elif kind == "dep" and i >= SUMMED:
+                nc.vector.scalar_tensor_tensor(tile[:], tile[:], gain_col(i), res_t[i][:], MULT, ADD)
+            elif kind == "arr" and i >= SUMMED:
                 nc.vector.scalar_tensor_tensor(z_plane(i), tile[:], gain_col(i), silu_tile(where[("dep", i)])[:], MULT, ADD)
 
         def add_term(i, hb, src, first, final):
@@ -340,6 +348,13 @@ def tile_list_parish_migration_pages_kernel(
                 )
 
         def round_sum(i, hb):
+            if i >= PACK:
+                pairs = later("z_pairs", [P, T2 * 2], BF16, "wa_wide1")
+                nc.scalar.copy(
+                    pairs[:].rearrange("p (w e) -> p w e", e=2)[:, hb * BANK : (hb + 1) * BANK, i - PACK],
+                    sum_banks[2 * (i % 2) + hb][:],
+                )
+                return
             nc.scalar.copy(
                 z_rows[hb][:, :, :, 64 * i : 64 * (i + 1)].rearrange("p b u (q e) -> p b u q e", e=2),
                 sum_banks[2 * (i % 2) + hb][:].rearrange("p (b q u e) -> p b u q e", b=4, u=2, e=2),
@@ -382,19 +397,28 @@ def tile_list_parish_migration_pages_kernel(
                     start=(g == 0 and t % 2 == 0), stop=(g == RP - 1 and t % 2 == 1),
                 )
 
-        def finish_sum(i):
-            terms = [silu_tile(where[(kind, i)]) for kind in ("dep", "arr")]
-            if i < RES_BY_TRANSPOSE:
-                terms = [res_t[i]] + terms
+        def open_sum(i):
             for hb in range(HALVES):
-                for n, src in enumerate(terms):
-                    add_term(i, hb, src, n == 0, n == len(terms) - 1)
+                add_term(i, hb, res_t[i], True, False)
+                add_term(i, hb, silu_tile(where[("dep", i)]), False, False)
+
+        def finish_sum(i):
+            for hb in range(HALVES):
+                add_term(i, hb, silu_tile(where[("arr", i)]), False, True)
                 round_sum(i, hb)
-            if i < RES_BY_TRANSPOSE:
-                load_res(i + RES_RING)
             if i == PACK - 1:
                 for q in range(CHUNKS):
                     interleave_z(q, word_banks[q % 2])
+            if i == SUMMED - 1:
+                words = made["z_pairs"][:].bitcast(F32)
+                for hb in range(HALVES):
+                    for b in range(4):
+                        m0 = (4 * hb + b) * P
+                        nc.tensor.transpose(word_banks[hb][:, b * P : (b + 1) * P], words[:, m0 : m0 + P], ident[:])
+                    nc.scalar.copy(
+                        z_in[:].bitcast(F32).rearrange("p (m u) -> p m u", u=2)[:, hb * BANK : (hb + 1) * BANK, 0],
+                        word_banks[hb][:],
+                    )
 
         issued = [1]
         casts = (lambda: cast_wa(1), cast_wo)
@@ -402,6 +426,13 @@ def tile_list_parish_migration_pages_kernel(
             lambda: quantize_wa(0), lambda: quantize_wa(1), quantize_wide,
             lambda: nc.vector.quantize_mx(out=wo_codes[:].bitcast(E4M3), scales=wo_sc[:], in_=made["wo_stage"][:]),
         )
+        def products_up_to(j):
+            for ahead in range(issued[0], min(j + AHEAD, last) + 1):
+                if j < NEEDS.get(ahead, 0):
+                    break
+                product(ahead)
+                issued[0] = ahead + 1
+
         cast_wa(0)
         product(0)
         for j in range(last):
@@ -415,24 +446,21 @@ def tile_list_parish_migration_pages_kernel(
                 deal_wd()
             if j > 0:
                 combine(j - 1)
-            for ahead in range(issued[0], min(j + AHEAD, last) + 1):
-                if j < NEEDS.get(ahead, 0):
-                    break
-                product(ahead)
-                issued[0] = ahead + 1
+            if j < TIGHT_FROM:
+                products_up_to(j)
+            activate(j)
+            products_up_to(j)
             if j in CAST_STEPS:
                 casts[CAST_STEPS.index(j)]()
-            if j == last - 1:
-                weave(nc.scalar.copy, 0, T2, 0, 2)
-            activate(j)
             if WIDE_STEP <= j < WIDE_STEP + KP:
                 cast_wide(j - WIDE_STEP)
-            if j > 0 and steps[j - 1][0] == "arr" and steps[j - 1][1] < PACK:
-                finish_sum(steps[j - 1][1])
-            if j == QUANTIZE_STEPS[-1]:
-                for q in range(CHUNKS):
-                    y_pass(0, q)
+            if j in SUM_STEPS:
+                finish_sum(SUM_STEPS.index(j))
+            if j in OPEN_STEPS:
+                open_sum(OPEN_STEPS.index(j))
 
+        for q in (0, 1, 3, 2):
+            y_pass(0, q)
         scatter(last)
         combine(last - 1)
         i = TILES - 1
@@ -449,14 +477,15 @@ def tile_list_parish_migration_pages_kernel(
         codes_view = out_1[0].rearrange("p m t -> p (m t)").bitcast(I32)
         y_sc = sb("y_sc", [P, T2], U8)
         y_codes = [sb(f"y_codes{q}", [P, QUART], U32) for q in range(CHUNKS)]
-        y_sb = [sb(f"y_sb{h}", [P, 2 * PACK * QUART], F32, tag=("wa_wide1", "big0")[h]) for h in range(2)]
+        y_sb = [sb(f"y_sb{h}", [P, 2 * PACK * QUART], F32, tag=("wa_wide2", "big0")[h]) for h in range(2)]
         for q in range(CHUNKS):
             cols = slice(q * QUART, (q + 1) * QUART)
             rows = y_sb[q // 2][:, (q % 2) * PACK * QUART : (q % 2 + 1) * PACK * QUART]
             rounded = z_rows[q // 2][:].rearrange("p b u w -> p (b u w)")[:, (q % 2) * PACK * QUART : (q % 2 + 1) * PACK * QUART]
             for s in range(2):
-                nc.scalar.copy(rows[:, s * BANK : (s + 1) * BANK], y_banks[q][s][:])
-            nc.sync.dma_start(out=y_view[:, :, cols], in_=rows.rearrange("p (t m) -> p t m", t=PACK))
+                half = rows[:, s * BANK : (s + 1) * BANK]
+                nc.scalar.copy(half, y_banks[q][s][:])
+                nc.sync.dma_start(out=y_view[:, 2 * s : 2 * s + 2, cols], in_=half.rearrange("p (t m) -> p t m", t=2))
             nc.vector.tensor_copy(
                 rounded.rearrange("p (c i t) -> p c t i", i=PACK, t=PACK),
                 rows.rearrange("p (t c i) -> p c t i", i=PACK, t=PACK),

@@ -30,27 +30,29 @@ QUART = 256
 CHUNKS = T2 // QUART
 WA_COLS = 256
 WA_CHUNKS = PASS // WA_COLS
+SCALE_ROWS = 16
+FIRST_TAGS = ("list", "big", "picked", "v_", "wd_sc", "wd_pair0", "page", "ident", "gain_dealt")
 RES_RING = 4
 H_RING = 3
 AHEAD = 2
 OPEN_STEPS = (2, 3, 6, 7, 10, 11)
 TIGHT_FROM = 9
-SUM_STEPS = (4, 5, 8, 9, 12, 13)
-GAIN_ON_VECTOR = (4, 5, 6, 7, 8, 9)
+SUM_STEPS = (5, 6, 8, 9, 12, 13)
+GAIN_ON_VECTOR = (5, 6, 7, 8, 9)
 SUMMED = 6
 WIDE_RING = 8
 GAIN_RUN = 13
 CAST_STEPS = (0, 8)
 WIDE_STEP = 4
-NEEDS = {1: 0, 4: 2, 8: 4, 11: 9}
-WEIGHED_FIRST = 2
-QUANTIZE_STEPS = (0, 2, 9, 11)
+NEEDS = {3: 1, 5: 3, 8: 5, 11: 9}
+WEIGHED_FIRST = 1
+QUANTIZE_STEPS = (1, 3, 9, 11)
 Z0_STEP = 11
-DEAL_STEP = 4
+DEAL_STEP = 5
 
 
 def step_order():
-    steps = [(kind, 2 * c + h) for c in range(WA_CHUNKS) for kind in ("dep", "arr") for h in range(2)]
+    steps = [("dep", 0), ("dep", 1), ("dep", 2), ("arr", 0), ("arr", 1), ("dep", 3), ("arr", 2), ("arr", 3)]
     return steps + [("dep", 4), ("dep", 5), ("dep", 6), ("arr", 4), ("arr", 5), ("dep", 7), ("arr", 6), ("arr", 7)]
 
 
@@ -63,8 +65,12 @@ def tile_list_parish_migration_pages_kernel(
         keep = ctx.enter_context(tc.tile_pool(name="keep", bufs=1))
         psum = ctx.enter_context(tc.psum_pool(name="psum", bufs=1))
 
+        pools = {"first": keep}
+
         def sb(name, shape, dtype, tag=None):
-            return keep.tile(shape, dtype, name=name, tag=tag or name, align_bytes=64)
+            tag = tag or name
+            pool = pools["first" if tag.startswith(FIRST_TAGS) else "later"]
+            return pool.tile(shape, dtype, name=name, tag=tag, align_bytes=64)
 
         made = {}
 
@@ -79,25 +85,21 @@ def tile_list_parish_migration_pages_kernel(
         list_t = sb("list_t", [P, S // 16], U16)
         lists = {"arr": sb("list_a", [P, S // 16], U16), "dep": sb("list_d", [P, S // 16], U16)}
         table = [sb(f"table{a}", [P, T], I32, tag=f"big{a}") for a in range(KP)]
-        table_sc = sb("table_sc", [P, KP, T], U8)
-        wd_sc = sb("wd_sc", [P, KP, H], U8)
-        wd_raw = [sb(f"wd_raw{g}", [P, KP, 2 * PASS], U8) for g in range(RP)]
-        wg = {kind: sb("wg_" + kind, [P, S], F32) for kind in ("arr", "dep")}
-        wg_dealt = {kind: [sb(f"wg_{kind}{t}", [P, S], F32) for t in range(PACK)] for kind in ("arr", "dep")}
-        wa_raw = [[sb(f"wa_raw{c}_{a}", [P, PACK * WA_COLS], F32) for a in range(KP)] for c in range(WA_CHUNKS)]
-        wa_wide = [sb(f"wa_wide{a}", [P, PACK * PASS], F32) for a in range(KP)]
-        res_t = [sb(f"res{b}", [P, T2], F32) for b in range(RES_RING)]
+        picked_sc = sb("picked_sc", [P, S], U8)
+        v_sc = sb("v_sc", [P, KP, S], U8)
+        wd_sc_raw = sb("wd_sc_raw", [P, KP, PASS], U8)
+        wd_sc = sb("wd_sc", [P, KP * PASS], U8)
+        wd_pairs = [sb("wd_pair0", [P, KP, 2 * WA_COLS], U8)]
         pages = {kind: [sb(f"page_{kind}{b}", [P, T2], F32) for b in range(2)] for kind in ("dep", "arr")}
         ident = sb("ident", [P, P], F32)
-        gain_t = sb("gain_t", [P, PACK], F32)
         gain_dealt = sb("gain_dealt", [P, 16], F32)
 
         def dealt(rows, t):
             return rows.rearrange("(c t i) w -> t c i w", t=PACK, i=PACK)[t]
 
-        def load_wd(g):
-            cols = wd_words.rearrange("a p c -> p a c")[:, :, g * 2 * PASS : (g + 1) * 2 * PASS]
-            nc.sync.dma_start(out=wd_raw[g][:].bitcast(I32), in_=cols.bitcast(I32))
+        def load_wd(dst, lo, hi):
+            cols = wd_words.rearrange("a p c -> p a c")[:, :, 2 * lo : 2 * hi]
+            nc.sync.dma_start(out=dst[:].bitcast(I32), in_=cols.bitcast(I32))
 
         def load_wa(dst, a, lo, hi):
             nc.sync.dma_start(
@@ -116,59 +118,77 @@ def tile_list_parish_migration_pages_kernel(
         def load_table(a):
             nc.sync.dma_start(out=table[a][:], in_=tab_words[a].rearrange("p t i -> p (t i)").bitcast(I32))
 
-        def load_scale_rows(dst, src):
+        def load_scale_rows(queue, dst, src):
             rows = src.rearrange("a (q r) c -> r q a c", r=4)
             for r in range(4):
-                nc.scalar.dma_start(out=dst[r:P:32, :, :].bitcast(I32), in_=rows[r].bitcast(I32))
+                queue.dma_start(out=dst[r:P:32, :, :].bitcast(I32), in_=rows[r].bitcast(I32))
 
         gain_view = gain[PASS:].rearrange("(c x) -> c x", x=16)
 
         def load_gain_dealt(i):
             nc.sync.dma_start(out=gain_dealt[i:P:PACK, 0:GAIN_RUN], in_=gain_view[:, i : i + GAIN_RUN])
 
-        sc_words = table_sc[:].rearrange("p a c -> p (a c)").bitcast(I32)
-        half_words = KP * T // 8
-        nc.vector.memset(sc_words[:, :half_words], 0)
-        nc.gpsimd.memset(sc_words[:, half_words:], 0)
-        nc.gpsimd.memset(wd_sc[:].rearrange("p a c -> p (a c)").bitcast(I32), 0)
-        nc.sync.dma_start(list_t[:], offs)
-        nc.sync.dma_start(lists["dep"][:], offs3)
-        nc.sync.dma_start(lists["arr"][:], offs2)
-        with nc.allow_non_contiguous_dma(reason="one gain for each row of a tile, on its partition"):
-            nc.sync.dma_start(out=gain_t[:], in_=gain[0:PASS].rearrange("(i p) -> p i", p=P))
-        load_gain_dealt(0)
-        load_gain_dealt(1)
-        load_table(0)
-        load_table(1)
-        load_scale_rows(table_sc, tab_scales)
-        load_wd(0)
-        load_table(2)
-        load_scale_rows(wd_sc, wd_scales)
+        with tc.tile_pool(name="window", bufs=1) as window_pool:
+            table_sc = window_pool.tile([P, T], U8, name="table_sc", align_bytes=64)
+            nc.vector.memset(table_sc[:].bitcast(I32), 0)
+            nc.gpsimd.memset(wd_sc[:].bitcast(I32), 0)
+            nc.vector.memset(v_sc[:].rearrange("p a c -> p (a c)").bitcast(I32), 0)
+            nc.sync.dma_start(list_t[:], offs)
+            nc.sync.dma_start(lists["dep"][:], offs3)
+            nc.sync.dma_start(lists["arr"][:], offs2)
+            load_scale_rows(nc.sync, wd_sc_raw, wd_scales[:, :, :PASS])
+            load_table(0)
+            nc.scalar.dma_start(
+                out=table_sc[0 : KP * SCALE_ROWS, :].bitcast(I32), in_=tab_scales.rearrange("a s t -> s a t").bitcast(I32)
+            )
+            for i in range(PACK):
+                load_gain_dealt(i)
+            load_table(1)
+            load_wd(wd_pairs[0], 0, WA_COLS)
+            load_table(2)
+            for q in range(4):
+                live = slice(32 * q, 32 * q + 4)
+                nc.vector.tensor_copy(
+                    wd_sc[live, :].bitcast(I32), wd_sc_raw[live, :, :].rearrange("p a c -> p (a c)").bitcast(I32)
+                )
+            nc.vector.tensor_copy(picked_sc[:], table_sc[:].indirect(list_t[:]))
+        for q in range(4):
+            nc.sync.dma_start(
+                out=v_sc[32 * q : 32 * q + 4, :, :].bitcast(I32), in_=picked_sc[4 * KP * q : 4 * KP * (q + 1), :].bitcast(I32)
+            )
+
+        pools["later"] = ctx.enter_context(tc.tile_pool(name="later", bufs=1))
+        gain_rows = sb("gain_rows", [P, P], F32)
+        late_sc = sb("late_sc", [P, KP, PASS], U8)
+        wd_pairs.append(sb("wd_pair1", [P, KP, 2 * WA_COLS], U8))
+        wd_wide = sb("wd_wide", [P, KP, 2 * PASS], U8)
+        wg = {kind: sb("wg_" + kind, [P, S], F32) for kind in ("arr", "dep")}
+        wg_dealt = {kind: [sb(f"wg_{kind}{t}", [P, S], F32) for t in range(PACK)] for kind in ("arr", "dep")}
+        wa_raw = [[sb(f"wa_raw{c}_{a}", [P, PACK * WA_COLS], F32) for a in range(KP)] for c in range(WA_CHUNKS)]
+        wa_wide = [sb(f"wa_wide{a}", [P, PACK * PASS], F32) for a in range(KP)]
+        res_t = [sb(f"res{b}", [P, T2], F32) for b in range(RES_RING)]
+        nc.gpsimd.memset(gain_rows[:], 0.0)
+        nc.gpsimd.memset(late_sc[:].rearrange("p a c -> p (a c)").bitcast(I32), 0)
         nc.sync.dma_start(out=wg["dep"][:], in_=wg2)
+        nc.sync.dma_start(out=gain_rows[0:PACK, :], in_=gain[0:PASS].rearrange("(i p) -> i p", p=P))
         for a in range(KP):
             load_wa(wa_raw[0][a], a, 0, WA_COLS)
+        load_wd(wd_pairs[1], WA_COLS, PASS)
         nc.sync.dma_start(out=wg["arr"][:], in_=wg1)
         for a in range(KP):
             load_wa(wa_raw[1][a], a, WA_COLS, PASS)
         load_res(0)
         load_res(1)
-        load_wd(1)
+        load_wd(wd_wide, PASS, H)
+        load_scale_rows(nc.sync, late_sc, wd_scales[:, :, PASS:])
         for a in range(KP):
             load_wa(wa_wide[a], a, PASS, H)
             if a > 0:
                 load_res(1 + a)
-        load_gain_dealt(2)
-        load_gain_dealt(3)
 
-        v_sc = sb("v_sc", [P, KP, S], U8)
-        v_first = sb("v_first", [P, S], U32)
-        nc.vector.tensor_copy(v_first[:], table[0][:].bitcast(U32).indirect(list_t[:]))
+        v_words = [sb(f"v_words{a}", [P, S], U32) for a in range(KP)]
         for a in range(KP):
-            nc.vector.tensor_copy(v_sc[:, a, :], table_sc[:, a, :].indirect(list_t[:]))
-        v_rest = sb("v_rest", [P, (KP - 1) * S], U32, tag="table_sc")
-        v_words = [v_first[:]] + [v_rest[:, a * S : (a + 1) * S] for a in range(KP - 1)]
-        for a in range(1, KP):
-            nc.vector.tensor_copy(v_words[a], table[a][:].bitcast(U32).indirect(list_t[:]))
+            nc.vector.tensor_copy(v_words[a][:], table[a][:].bitcast(U32).indirect(list_t[:]))
         for page in pages["dep"]:
             nc.gpsimd.memset(page[:], 0.0)
         make_identity(nc, ident[:])
@@ -221,15 +241,14 @@ def tile_list_parish_migration_pages_kernel(
                 )
 
         def deal_wd():
+            nc.vector.tensor_copy(
+                later("wd_dealt_sc", [P, PACK * KP * P], U8, "stage0")[:].bitcast(I32).rearrange("p (t a c) -> p a c t", t=PACK, a=KP),
+                late_sc[:].bitcast(I32).rearrange("p a (c t) -> p a c t", t=PACK),
+            )
             wd_codes = later("wd_codes", [P, PACK * KP * 2 * P], U8, "stage1")
-            wd_sc_dealt = later("wd_sc_dealt", [P, PACK * KP * P], U8, "stage0")
             nc.vector.tensor_copy(
                 wd_codes[:].bitcast(I32).rearrange("p (t a c w) -> p a c t w", t=PACK, a=KP, w=2),
-                wd_raw[1][:].bitcast(I32).rearrange("p a (c t w) -> p a c t w", t=PACK, w=2),
-            )
-            nc.vector.tensor_copy(
-                wd_sc_dealt[:].bitcast(I32).rearrange("p (t a c) -> p a c t", t=PACK, a=KP),
-                wd_sc[:, :, PASS:].bitcast(I32).rearrange("p a (c t) -> p a c t", t=PACK),
+                wd_wide[:].bitcast(I32).rearrange("p a (c t w) -> p a c t w", t=PACK, w=2),
             )
 
         def cast_wide(a):
@@ -257,11 +276,11 @@ def tile_list_parish_migration_pages_kernel(
                     )
 
         def h_tile(j):
-            return later(f"h_step{j}", [P, S], F32, {Z0_STEP: "pin_z", WIDE_STEP - 1: "pin_wide", 0: "pin_wa0", 1: "stage0", 2: "pin_wa1", 4: "stage1"}.get(j, f"h{j % H_RING}"))
+            return later(f"h_step{j}", [P, S], F32, {Z0_STEP: "pin_z", WIDE_STEP - 1: "pin_wide", 0: "pin_wa0", 2: "pin_wa1", 5: "stage1"}.get(j, f"h{j % H_RING}"))
 
         silu_tags = {
-            0: "wa_raw0_2", 1: "wa_raw1_2", 2: "wa_raw0_1", 3: "wa_raw0_0", 4: "wa_raw1_0", 5: "wa_raw1_1",
-            6: "big2", 7: "wd_raw0", 8: "wa_wide2", 9: "big1", 15: "wa_wide1",
+            0: "wa_raw0_2", 1: "wa_raw1_2", 2: "silu_spare", 3: "wa_raw0_0", 4: "wa_raw1_0", 5: "wa_raw1_1",
+            6: "big2", 7: "wd_sc_raw", 8: "wa_wide2", 9: "big1", 15: "wa_wide1",
         }
         silu_again = {11: 0, 10: 1, 12: 2, 13: 3, 14: 4}
 
@@ -271,7 +290,7 @@ def tile_list_parish_migration_pages_kernel(
 
         def page_of(j):
             kind, i = steps[j]
-            return pages[kind][i % 2]
+            return pages[kind][(i + ((kind, i) == ("dep", 3))) % 2]
 
         def gain_col(i):
             return gain_t[:, i : i + 1] if i < PACK else gain_dealt[:, PACK * (i - PACK) : PACK * (i - PACK) + 1]
@@ -292,14 +311,14 @@ def tile_list_parish_migration_pages_kernel(
                     cols = slice(a * PASS + t * P, a * PASS + (t + 1) * P)
                     lhs, lhs_sc = wide_codes[:, cols].bitcast(E4M3), wide_sc[:, cols]
                 elif i < PACK:
-                    lhs = wd_raw[0][:, a, i * 2 * P : (i + 1) * 2 * P].bitcast(E2M1)
-                    lhs_sc = wd_sc[:, a, i * P : (i + 1) * P]
+                    lhs = wd_pairs[i // 2][:, a, (i % 2) * 2 * P : (i % 2 + 1) * 2 * P].bitcast(E2M1)
+                    lhs_sc = wd_sc[:, a * PASS + i * P : a * PASS + (i + 1) * P]
                 else:
                     n = t * KP + a
                     lhs = made["wd_codes"][:, n * 2 * P : (n + 1) * 2 * P].bitcast(E2M1)
-                    lhs_sc = made["wd_sc_dealt"][:, n * P : (n + 1) * P]
+                    lhs_sc = made["wd_dealt_sc"][:, n * P : (n + 1) * P]
                 nc.tensor.matmul_mx(
-                    out=bank[:], lhsT=lhs, lhsT_scale=lhs_sc, rhs=v_words[a].bitcast(E4M3),
+                    out=bank[:], lhsT=lhs, lhsT_scale=lhs_sc, rhs=v_words[a][:].bitcast(E4M3),
                     rhs_scale=v_sc[:, a, :], start=(a == 0), stop=(a == KP - 1),
                 )
             if j < WEIGHED_FIRST:
@@ -420,7 +439,7 @@ def tile_list_parish_migration_pages_kernel(
                         word_banks[hb][:],
                     )
 
-        issued = [1]
+        issued = [2]
         casts = (lambda: cast_wa(1), cast_wo)
         quantizers = (
             lambda: quantize_wa(0), lambda: quantize_wa(1), quantize_wide,
@@ -435,6 +454,10 @@ def tile_list_parish_migration_pages_kernel(
 
         cast_wa(0)
         product(0)
+        product(1)
+        gain_t = sb("gain_t", [P, PACK], F32, tag="wa_raw0_1")
+        nc.tensor.transpose(h_banks[0][:, 0:P], gain_rows[:], ident[:])
+        nc.scalar.copy(gain_t[:], h_banks[0][:, 0:PACK])
         for j in range(last):
             scatter(j)
             if j in QUANTIZE_STEPS:

@@ -169,10 +169,11 @@ def tile_list_parish_migration_pages_kernel(
         res_t = [sb(f"res{b}", [P, T2], F32) for b in range(RES_RING)]
         nc.gpsimd.memset(gain_rows[:], 0.0)
         nc.gpsimd.memset(late_sc[:].rearrange("p a c -> p (a c)").bitcast(I32), 0)
-        nc.sync.dma_start(out=wg["dep"][:], in_=wg2)
-        nc.sync.dma_start(out=gain_rows[0:PACK, :], in_=gain[0:PASS].rearrange("(i p) -> i p", p=P))
         for a in range(KP):
             load_wa(wa_raw[0][a], a, 0, WA_COLS)
+            if a == 0:
+                nc.sync.dma_start(out=wg["dep"][:], in_=wg2)
+        nc.sync.dma_start(out=gain_rows[0:PACK, :], in_=gain[0:PASS].rearrange("(i p) -> i p", p=P))
         load_wd(wd_pairs[1], WA_COLS, PASS)
         nc.sync.dma_start(out=wg["arr"][:], in_=wg1)
         for a in range(KP):
@@ -241,14 +242,14 @@ def tile_list_parish_migration_pages_kernel(
                 )
 
         def deal_wd():
+            wd_dealt = later("wd_dealt", [P, PACK * KP * 3 * P], U8, "stage0")
             nc.vector.tensor_copy(
-                later("wd_dealt_sc", [P, PACK * KP * P], U8, "stage0")[:].bitcast(I32).rearrange("p (t a c) -> p a c t", t=PACK, a=KP),
-                late_sc[:].bitcast(I32).rearrange("p a (c t) -> p a c t", t=PACK),
-            )
-            wd_codes = later("wd_codes", [P, PACK * KP * 2 * P], U8, "stage1")
-            nc.vector.tensor_copy(
-                wd_codes[:].bitcast(I32).rearrange("p (t a c w) -> p a c t w", t=PACK, a=KP, w=2),
+                wd_dealt[:, : PACK * KP * 2 * P].bitcast(I32).rearrange("p (t a c w) -> p a c t w", t=PACK, a=KP, w=2),
                 wd_wide[:].bitcast(I32).rearrange("p a (c t w) -> p a c t w", t=PACK, w=2),
+            )
+            nc.vector.tensor_copy(
+                wd_dealt[:, PACK * KP * 2 * P :].bitcast(I32).rearrange("p (t a c) -> p a c t", t=PACK, a=KP),
+                late_sc[:].bitcast(I32).rearrange("p a (c t) -> p a c t", t=PACK),
             )
 
         def cast_wide(a):
@@ -276,7 +277,7 @@ def tile_list_parish_migration_pages_kernel(
                     )
 
         def h_tile(j):
-            return later(f"h_step{j}", [P, S], F32, {Z0_STEP: "pin_z", WIDE_STEP - 1: "pin_wide", 0: "pin_wa0", 2: "pin_wa1", 5: "stage1"}.get(j, f"h{j % H_RING}"))
+            return later(f"h_step{j}", [P, S], F32, {Z0_STEP - 1: "pin_z", WIDE_STEP - 1: "pin_wide", 0: "pin_wa0", 2: "pin_wa1", 5: "stage1"}.get(j, f"h{j % H_RING}"))
 
         silu_tags = {
             0: "wa_raw0_2", 1: "wa_raw1_2", 2: "silu_spare", 3: "wa_raw0_0", 4: "wa_raw1_0", 5: "wa_raw1_1",
@@ -295,8 +296,8 @@ def tile_list_parish_migration_pages_kernel(
         def gain_col(i):
             return gain_t[:, i : i + 1] if i < PACK else gain_dealt[:, PACK * (i - PACK) : PACK * (i - PACK) + 1]
 
-        def z_plane(i):
-            return later("z_planes", [P, PACK * T2], BF16, "wa_wide0")[:, (i - PACK) * T2 : (i - PACK + 1) * T2]
+        def z_planes(hb):
+            return later(f"z_planes{hb}", [P, 2 * BANK], BF16, "wa_wide0")
 
         def product(j):
             kind, i = steps[j]
@@ -315,8 +316,8 @@ def tile_list_parish_migration_pages_kernel(
                     lhs_sc = wd_sc[:, a * PASS + i * P : a * PASS + (i + 1) * P]
                 else:
                     n = t * KP + a
-                    lhs = made["wd_codes"][:, n * 2 * P : (n + 1) * 2 * P].bitcast(E2M1)
-                    lhs_sc = made["wd_dealt_sc"][:, n * P : (n + 1) * P]
+                    lhs = made["wd_dealt"][:, n * 2 * P : (n + 1) * 2 * P].bitcast(E2M1)
+                    lhs_sc = made["wd_dealt"][:, (2 * PACK * KP + n) * P : (2 * PACK * KP + n + 1) * P]
                 nc.tensor.matmul_mx(
                     out=bank[:], lhsT=lhs, lhsT_scale=lhs_sc, rhs=v_words[a][:].bitcast(E4M3),
                     rhs_scale=v_sc[:, a, :], start=(a == 0), stop=(a == KP - 1),
@@ -342,9 +343,10 @@ def tile_list_parish_migration_pages_kernel(
             if i >= SUMMED or j in GAIN_ON_VECTOR:
                 nc.scalar.activation(tile[:], page_of(j)[:], ACT.Silu)
                 return
-            for cols in halves:
+            parts = halves if i >= PACK else [slice(0, T2)]
+            for cols in parts:
                 nc.scalar.activation(tile[:, cols], page_of(j)[:, cols], ACT.Silu)
-            for cols in halves:
+            for cols in parts:
                 nc.scalar.activation(tile[:, cols], tile[:, cols], ACT.Copy, scale=gain_col(i))
 
         def combine(j):
@@ -354,8 +356,6 @@ def tile_list_parish_migration_pages_kernel(
                 nc.vector.tensor_scalar(tile[:], tile[:], gain_col(i), None, MULT)
             elif kind == "dep" and i >= SUMMED:
                 nc.vector.scalar_tensor_tensor(tile[:], tile[:], gain_col(i), res_t[i][:], MULT, ADD)
-            elif kind == "arr" and i >= SUMMED:
-                nc.vector.scalar_tensor_tensor(z_plane(i), tile[:], gain_col(i), silu_tile(where[("dep", i)])[:], MULT, ADD)
 
         def add_term(i, hb, src, first, final):
             bank = sum_banks[2 * (i % 2) + hb]
@@ -391,11 +391,11 @@ def tile_list_parish_migration_pages_kernel(
                 bank[:].rearrange("p (b u m) -> p b m u", b=2, u=2),
             )
 
-        def weave(copy, lo, hi, t0, t1):
-            c0, c1 = lo // PACK, hi // PACK
-            copy(
-                z_in[:].rearrange("p (c i t) -> p c t i", i=PACK, t=PACK)[:, c0:c1, t0:t1, :],
-                made["z_planes"][:].rearrange("p (t c i) -> p c t i", i=PACK, t=PACK)[:, c0:c1, t0:t1, :],
+        def weave(q):
+            hb, c0 = q // 2, (q % 2) * QUART // PACK
+            nc.vector.tensor_copy(
+                z_in[:, q * PACK * QUART : (q + 1) * PACK * QUART].rearrange("p (c i t) -> p c t i", i=PACK, t=PACK)[:, :, 2:PACK, :],
+                z_planes(hb)[:].rearrange("p (t c i) -> p c t i", i=PACK, t=2)[:, c0 : c0 + QUART // PACK, :, :],
             )
 
         def quantize_z(g, lo, hi):
@@ -485,15 +485,17 @@ def tile_list_parish_migration_pages_kernel(
         for q in (0, 1, 3, 2):
             y_pass(0, q)
         scatter(last)
-        combine(last - 1)
         i = TILES - 1
-        mine, other = silu_tile(last), silu_tile(where[("dep", i)])
+        mine = silu_tile(last)
         quarters = [slice(q * QUART, (q + 1) * QUART) for q in range(CHUNKS)]
         for cols in quarters:
             nc.scalar.activation(mine[:, cols], page_of(last)[:, cols], ACT.Silu)
         for q, cols in enumerate(quarters):
-            nc.vector.scalar_tensor_tensor(z_plane(i)[:, cols], mine[:, cols], gain_col(i), other[:, cols], MULT, ADD)
-            weave(nc.vector.tensor_copy, q * QUART, (q + 1) * QUART, 2, PACK)
+            for n in (i - 1, i):
+                arr, dep = silu_tile(where[("arr", n)]), silu_tile(where[("dep", n)])
+                lo = (n - SUMMED) * BANK + (q % 2) * QUART
+                nc.vector.scalar_tensor_tensor(z_planes(q // 2)[:, lo : lo + QUART], arr[:, cols], gain_col(n), dep[:, cols], MULT, ADD)
+            weave(q)
             quantize_z(1, q * QUART, (q + 1) * QUART)
             y_pass(1, q)
         y_view = out_0.rearrange("(p t) m -> p t m", t=PACK)

@@ -31,7 +31,7 @@ CHUNKS = T2 // QUART
 WA_COLS = 256
 WA_CHUNKS = PASS // WA_COLS
 SCALE_ROWS = 16
-FIRST_TAGS = ("list", "big", "picked", "v_", "wd_sc", "wd_pair0", "page", "ident", "gain_dealt")
+FIRST_TAGS = ("list", "big", "picked", "v_", "wd_sc", "wd_pair0", "gain_dealt")
 RES_RING = 4
 H_RING = 3
 AHEAD = 2
@@ -90,8 +90,6 @@ def tile_list_parish_migration_pages_kernel(
         wd_sc_raw = sb("wd_sc_raw", [P, KP, PASS], U8)
         wd_sc = sb("wd_sc", [P, KP * PASS], U8)
         wd_pairs = [sb("wd_pair0", [P, KP, 2 * WA_COLS], U8)]
-        pages = {kind: [sb(f"page_{kind}{b}", [P, T2], F32) for b in range(2)] for kind in ("dep", "arr")}
-        ident = sb("ident", [P, P], F32)
         gain_dealt = sb("gain_dealt", [P, 16], F32)
 
         def dealt(rows, t):
@@ -159,6 +157,8 @@ def tile_list_parish_migration_pages_kernel(
 
         pools["later"] = ctx.enter_context(tc.tile_pool(name="later", bufs=1))
         gain_rows = sb("gain_rows", [P, P], F32)
+        pages = {kind: [sb(f"page_{kind}{b}", [P, T2], F32) for b in range(2)] for kind in ("dep", "arr")}
+        ident = sb("ident", [P, P], F32)
         late_sc = sb("late_sc", [P, KP, PASS], U8)
         wd_pairs.append(sb("wd_pair1", [P, KP, 2 * WA_COLS], U8))
         wd_wide = sb("wd_wide", [P, KP, 2 * PASS], U8)

@@ -31,22 +31,22 @@ CHUNKS = T2 // QUART
 WA_COLS = 256
 WA_CHUNKS = PASS // WA_COLS
 SCALE_ROWS = 16
-FIRST_TAGS = ("list", "big", "picked", "v_", "wd_sc", "wd_pair0", "gain_dealt")
+FIRST_TAGS = ("list", "big", "picked", "v_", "wd_sc", "wd_pair0", "page", "ident", "gain_", "late_sc")
 RES_RING = 4
 H_RING = 3
 AHEAD = 2
 OPEN_STEPS = (2, 3, 6, 7, 10, 11)
 TIGHT_FROM = 9
 SUM_STEPS = (5, 6, 8, 9, 12, 13)
-GAIN_ON_VECTOR = (5, 6, 7, 8, 9)
+GAIN_ON_VECTOR = (5, 6, 7, 9)
 SUMMED = 6
 WIDE_RING = 8
 GAIN_RUN = 13
-CAST_STEPS = (0, 8)
+CAST_STEPS = (0, 8, 11)
 WIDE_STEP = 4
 NEEDS = {3: 1, 5: 3, 8: 5, 11: 9}
 WEIGHED_FIRST = 1
-QUANTIZE_STEPS = (1, 3, 9, 11)
+QUANTIZE_STEPS = (1, 3, 9, 11, 13)
 Z0_STEP = 11
 DEAL_STEP = 5
 
@@ -91,6 +91,10 @@ def tile_list_parish_migration_pages_kernel(
         wd_sc = sb("wd_sc", [P, KP * PASS], U8)
         wd_pairs = [sb("wd_pair0", [P, KP, 2 * WA_COLS], U8)]
         gain_dealt = sb("gain_dealt", [P, 16], F32)
+        pages = {"dep": [sb("page_dep0", [P, T2], F32)], "arr": []}
+        gain_rows = sb("gain_rows", [P, P], F32)
+        late_sc = sb("late_sc", [P, KP, PASS], U8)
+        ident = sb("ident", [P, P], F32)
 
         def dealt(rows, t):
             return rows.rearrange("(c t i) w -> t c i w", t=PACK, i=PACK)[t]
@@ -131,6 +135,10 @@ def tile_list_parish_migration_pages_kernel(
             nc.vector.memset(table_sc[:].bitcast(I32), 0)
             nc.gpsimd.memset(wd_sc[:].bitcast(I32), 0)
             nc.vector.memset(v_sc[:].rearrange("p a c -> p (a c)").bitcast(I32), 0)
+            nc.gpsimd.memset(gain_rows[:], 0.0)
+            make_identity(nc, ident[:])
+            nc.vector.memset(pages["dep"][0][:], 0.0)
+            nc.vector.memset(late_sc[:].rearrange("p a c -> p (a c)").bitcast(I32), 0)
             nc.sync.dma_start(list_t[:], offs)
             nc.sync.dma_start(lists["dep"][:], offs3)
             nc.sync.dma_start(lists["arr"][:], offs2)
@@ -156,10 +164,6 @@ def tile_list_parish_migration_pages_kernel(
             )
 
         pools["later"] = ctx.enter_context(tc.tile_pool(name="later", bufs=1))
-        gain_rows = sb("gain_rows", [P, P], F32)
-        pages = {kind: [sb(f"page_{kind}{b}", [P, T2], F32) for b in range(2)] for kind in ("dep", "arr")}
-        ident = sb("ident", [P, P], F32)
-        late_sc = sb("late_sc", [P, KP, PASS], U8)
         wd_pairs.append(sb("wd_pair1", [P, KP, 2 * WA_COLS], U8))
         wd_wide = sb("wd_wide", [P, KP, 2 * PASS], U8)
         wg = {kind: sb("wg_" + kind, [P, S], F32) for kind in ("arr", "dep")}
@@ -167,8 +171,6 @@ def tile_list_parish_migration_pages_kernel(
         wa_raw = [[sb(f"wa_raw{c}_{a}", [P, PACK * WA_COLS], F32) for a in range(KP)] for c in range(WA_CHUNKS)]
         wa_wide = [sb(f"wa_wide{a}", [P, PACK * PASS], F32) for a in range(KP)]
         res_t = [sb(f"res{b}", [P, T2], F32) for b in range(RES_RING)]
-        nc.gpsimd.memset(gain_rows[:], 0.0)
-        nc.gpsimd.memset(late_sc[:].rearrange("p a c -> p (a c)").bitcast(I32), 0)
         for a in range(KP):
             load_wa(wa_raw[0][a], a, 0, WA_COLS)
             if a == 0:
@@ -179,22 +181,24 @@ def tile_list_parish_migration_pages_kernel(
         for a in range(KP):
             load_wa(wa_raw[1][a], a, WA_COLS, PASS)
         load_res(0)
+        load_wa(wa_wide[0], 0, PASS, H)
         load_res(1)
         load_wd(wd_wide, PASS, H)
         load_scale_rows(nc.sync, late_sc, wd_scales[:, :, PASS:])
-        for a in range(KP):
+        for a in range(1, KP):
             load_wa(wa_wide[a], a, PASS, H)
-            if a > 0:
-                load_res(1 + a)
+        load_res(2)
+        load_res(3)
 
         v_words = [sb(f"v_words{a}", [P, S], U32) for a in range(KP)]
         for a in range(KP):
             nc.vector.tensor_copy(v_words[a][:], table[a][:].bitcast(U32).indirect(list_t[:]))
-        for page in pages["dep"]:
-            nc.gpsimd.memset(page[:], 0.0)
-        make_identity(nc, ident[:])
-        for page in pages["arr"]:
-            nc.gpsimd.memset(page[:], 0.0)
+
+        def clear_page(kind, tag):
+            pages[kind].append(sb(f"page_{kind}{len(pages[kind])}", [P, T2], F32, tag=tag))
+            nc.gpsimd.memset(pages[kind][-1][:], 0.0)
+
+        clear_page("dep", "picked_sc")
         wo_raw = [sb(f"wo_raw{g}", [P, PACK * N], F32, tag=f"big{g}") for g in range(RP)]
         nc.sync.dma_start(
             out=wo_raw[0][:].rearrange("p (j n) -> p j n", j=PACK), in_=wo[0:PASS, :].rearrange("(p j) n -> p j n", j=PACK)
@@ -266,24 +270,25 @@ def tile_list_parish_migration_pages_kernel(
                     in_=made["wide_stage"][:, PACK * lo : PACK * hi],
                 )
 
-        def cast_wo():
-            wo_stage = later("wo_stage", [P, RP * PACK * N], BF16, "wa_wide0")
-            for g in range(RP):
-                for s in range(2):
-                    lo = (2 * g + s) * 2 * PACK * P
-                    nc.scalar.copy(
-                        wo_stage[:, lo : lo + 2 * PACK * P].rearrange("p (t m j) -> p m j t", t=2, j=PACK),
-                        wo_raw[g][:].rearrange("p (j m t) -> p m j t", j=PACK, t=PACK)[:, :, :, 2 * s : 2 * s + 2],
-                    )
+        def cast_wo(g):
+            wo_stage = later(f"wo_stage{g}", [P, PACK * N], BF16, ("wa_wide0", "wa_wide2")[g])
+            nc.scalar.copy(
+                wo_stage[:].rearrange("p (t m j) -> p m j t", t=PACK, j=PACK),
+                wo_raw[g][:].rearrange("p (j m t) -> p m j t", j=PACK, t=PACK),
+            )
+
+        def quantize_wo(g):
+            cols = slice(g * N, (g + 1) * N)
+            nc.vector.quantize_mx(out=wo_codes[:, cols].bitcast(E4M3), scales=wo_sc[:, cols], in_=made[f"wo_stage{g}"][:])
 
         def h_tile(j):
             return later(f"h_step{j}", [P, S], F32, {Z0_STEP - 1: "pin_z", WIDE_STEP - 1: "pin_wide", 0: "pin_wa0", 2: "pin_wa1", 5: "stage1"}.get(j, f"h{j % H_RING}"))
 
         silu_tags = {
             0: "wa_raw0_2", 1: "wa_raw1_2", 2: "silu_spare", 3: "wa_raw0_0", 4: "wa_raw1_0", 5: "wa_raw1_1",
-            6: "big2", 7: "wd_sc_raw", 8: "wa_wide2", 9: "big1", 15: "wa_wide1",
+            6: "big2", 7: "wd_sc_raw", 8: "wa_wide2", 15: "wa_wide1",
         }
-        silu_again = {11: 0, 10: 1, 12: 2, 13: 3, 14: 4}
+        silu_again = {9: 5, 11: 0, 10: 1, 12: 2, 13: 3, 14: 4}
 
         def silu_tile(j):
             j = silu_again.get(j, j)
@@ -296,8 +301,8 @@ def tile_list_parish_migration_pages_kernel(
         def gain_col(i):
             return gain_t[:, i : i + 1] if i < PACK else gain_dealt[:, PACK * (i - PACK) : PACK * (i - PACK) + 1]
 
-        def z_planes(hb):
-            return later(f"z_planes{hb}", [P, 2 * BANK], BF16, "wa_wide0")
+        def z_words():
+            return later("z_words", [P, PACK * T2], BF16, "wa_wide0")
 
         def product(j):
             kind, i = steps[j]
@@ -343,7 +348,7 @@ def tile_list_parish_migration_pages_kernel(
             if i >= SUMMED or j in GAIN_ON_VECTOR:
                 nc.scalar.activation(tile[:], page_of(j)[:], ACT.Silu)
                 return
-            parts = halves if i >= PACK else [slice(0, T2)]
+            parts = halves if i >= PACK and kind == "arr" else [slice(0, T2)]
             for cols in parts:
                 nc.scalar.activation(tile[:, cols], page_of(j)[:, cols], ACT.Silu)
             for cols in parts:
@@ -358,9 +363,12 @@ def tile_list_parish_migration_pages_kernel(
                 nc.vector.scalar_tensor_tensor(tile[:], tile[:], gain_col(i), res_t[i][:], MULT, ADD)
 
         def add_term(i, hb, src, first, final):
-            bank = sum_banks[2 * (i % 2) + hb]
-            for b in range(4):
-                m0 = (4 * hb + b) * P
+            for n in range(4):
+                m0 = (4 * hb + n) * P
+                if i < PACK:
+                    bank, b = sum_banks[2 * (i % 2) + hb], n
+                else:
+                    bank, b = sum_banks[2 * hb + n // 2], 2 * (i - PACK) + n % 2
                 nc.tensor.matmul(
                     bank[:, b * P : (b + 1) * P], src[:, m0 : m0 + P], ident[:],
                     start=(first and b == 0), stop=(final and b == 3), is_transpose=True,
@@ -369,10 +377,11 @@ def tile_list_parish_migration_pages_kernel(
         def round_sum(i, hb):
             if i >= PACK:
                 pairs = later("z_pairs", [P, T2 * 2], BF16, "wa_wide1")
-                nc.scalar.copy(
-                    pairs[:].rearrange("p (w e) -> p w e", e=2)[:, hb * BANK : (hb + 1) * BANK, i - PACK],
-                    sum_banks[2 * (i % 2) + hb][:],
-                )
+                for k in range(2 * hb, 2 * hb + 2):
+                    nc.scalar.copy(
+                        pairs[:, k * BANK : (k + 1) * BANK].rearrange("p (w e) -> p w e", e=2),
+                        sum_banks[k][:].rearrange("p (e w) -> p w e", e=2),
+                    )
                 return
             nc.scalar.copy(
                 z_rows[hb][:, :, :, 64 * i : 64 * (i + 1)].rearrange("p b u (q e) -> p b u q e", e=2),
@@ -392,10 +401,11 @@ def tile_list_parish_migration_pages_kernel(
             )
 
         def weave(q):
-            hb, c0 = q // 2, (q % 2) * QUART // PACK
+            blocks = z_words()[:].bitcast(F32).rearrange("p (n m) -> p n m", m=QUART)
+            second = CHUNKS + q % 2
             nc.vector.tensor_copy(
-                z_in[:, q * PACK * QUART : (q + 1) * PACK * QUART].rearrange("p (c i t) -> p c t i", i=PACK, t=PACK)[:, :, 2:PACK, :],
-                z_planes(hb)[:].rearrange("p (t c i) -> p c t i", i=PACK, t=2)[:, c0 : c0 + QUART // PACK, :, :],
+                z_in[:].bitcast(F32)[:, 2 * q * QUART : 2 * (q + 1) * QUART].rearrange("p (m u) -> p m u", u=2),
+                blocks[:, q : second + 1 : second - q, :].rearrange("p u m -> p m u"),
             )
 
         def quantize_z(g, lo, hi):
@@ -418,13 +428,14 @@ def tile_list_parish_migration_pages_kernel(
 
         def open_sum(i):
             for hb in range(HALVES):
-                add_term(i, hb, res_t[i], True, False)
+                add_term(i, hb, res_t[i], i <= PACK, False)
                 add_term(i, hb, silu_tile(where[("dep", i)]), False, False)
 
         def finish_sum(i):
             for hb in range(HALVES):
-                add_term(i, hb, silu_tile(where[("arr", i)]), False, True)
-                round_sum(i, hb)
+                add_term(i, hb, silu_tile(where[("arr", i)]), False, i != PACK)
+                if i != PACK:
+                    round_sum(i, hb)
             if i == PACK - 1:
                 for q in range(CHUNKS):
                     interleave_z(q, word_banks[q % 2])
@@ -434,16 +445,13 @@ def tile_list_parish_migration_pages_kernel(
                     for b in range(4):
                         m0 = (4 * hb + b) * P
                         nc.tensor.transpose(word_banks[hb][:, b * P : (b + 1) * P], words[:, m0 : m0 + P], ident[:])
-                    nc.scalar.copy(
-                        z_in[:].bitcast(F32).rearrange("p (m u) -> p m u", u=2)[:, hb * BANK : (hb + 1) * BANK, 0],
-                        word_banks[hb][:],
-                    )
+                    nc.scalar.copy(z_words()[:].bitcast(F32)[:, hb * BANK : (hb + 1) * BANK], word_banks[hb][:])
 
         issued = [2]
-        casts = (lambda: cast_wa(1), cast_wo)
+        casts = (lambda: cast_wa(1), lambda: cast_wo(0), lambda: cast_wo(1))
         quantizers = (
             lambda: quantize_wa(0), lambda: quantize_wa(1), quantize_wide,
-            lambda: nc.vector.quantize_mx(out=wo_codes[:].bitcast(E4M3), scales=wo_sc[:], in_=made["wo_stage"][:]),
+            lambda: quantize_wo(0), lambda: quantize_wo(1),
         )
         def products_up_to(j):
             for ahead in range(issued[0], min(j + AHEAD, last) + 1):
@@ -458,6 +466,8 @@ def tile_list_parish_migration_pages_kernel(
         gain_t = sb("gain_t", [P, PACK], F32, tag="wa_raw0_1")
         nc.tensor.transpose(h_banks[0][:, 0:P], gain_rows[:], ident[:])
         nc.scalar.copy(gain_t[:], h_banks[0][:, 0:PACK])
+        clear_page("arr", "wd_pair0")
+        clear_page("arr", "gain_rows")
         for j in range(last):
             scatter(j)
             if j in QUANTIZE_STEPS:
@@ -493,8 +503,9 @@ def tile_list_parish_migration_pages_kernel(
         for q, cols in enumerate(quarters):
             for n in (i - 1, i):
                 arr, dep = silu_tile(where[("arr", n)]), silu_tile(where[("dep", n)])
-                lo = (n - SUMMED) * BANK + (q % 2) * QUART
-                nc.vector.scalar_tensor_tensor(z_planes(q // 2)[:, lo : lo + QUART], arr[:, cols], gain_col(n), dep[:, cols], MULT, ADD)
+                lo = 2 * (CHUNKS + q % 2) * QUART
+                pair = z_words()[:, lo : lo + 2 * QUART].rearrange("p (m e) -> p e m", e=2)[:, n - SUMMED, :]
+                nc.vector.scalar_tensor_tensor(pair, arr[:, cols], gain_col(n), dep[:, cols], MULT, ADD)
             weave(q)
             quantize_z(1, q * QUART, (q + 1) * QUART)
             y_pass(1, q)

@@ -31,7 +31,7 @@ CHUNKS = T2 // QUART
 WA_COLS = 256
 WA_CHUNKS = PASS // WA_COLS
 SCALE_ROWS = 16
-FIRST_TAGS = ("list", "big", "picked", "v_", "wd_sc", "wd_pair0", "page", "ident", "gain_", "late_sc")
+FIRST_TAGS = ("list", "big", "picked", "v_", "wd_sc", "wd_pair0", "ident", "gain_dealt")
 RES_RING = 4
 H_RING = 3
 AHEAD = 2
@@ -91,9 +91,7 @@ def tile_list_parish_migration_pages_kernel(
         wd_sc = sb("wd_sc", [P, KP * PASS], U8)
         wd_pairs = [sb("wd_pair0", [P, KP, 2 * WA_COLS], U8)]
         gain_dealt = sb("gain_dealt", [P, 16], F32)
-        pages = {"dep": [sb("page_dep0", [P, T2], F32)], "arr": []}
-        gain_rows = sb("gain_rows", [P, P], F32)
-        late_sc = sb("late_sc", [P, KP, PASS], U8)
+        pages = {"dep": [], "arr": []}
         ident = sb("ident", [P, P], F32)
 
         def dealt(rows, t):
@@ -133,12 +131,9 @@ def tile_list_parish_migration_pages_kernel(
         with tc.tile_pool(name="window", bufs=1) as window_pool:
             table_sc = window_pool.tile([P, T], U8, name="table_sc", align_bytes=64)
             nc.vector.memset(table_sc[:].bitcast(I32), 0)
-            nc.gpsimd.memset(wd_sc[:].bitcast(I32), 0)
-            nc.vector.memset(v_sc[:].rearrange("p a c -> p (a c)").bitcast(I32), 0)
-            nc.gpsimd.memset(gain_rows[:], 0.0)
             make_identity(nc, ident[:])
-            nc.vector.memset(pages["dep"][0][:], 0.0)
-            nc.vector.memset(late_sc[:].rearrange("p a c -> p (a c)").bitcast(I32), 0)
+            nc.vector.memset(wd_sc[:].bitcast(I32), 0)
+            nc.vector.memset(v_sc[:].rearrange("p a c -> p (a c)").bitcast(I32), 0)
             nc.sync.dma_start(list_t[:], offs)
             nc.sync.dma_start(lists["dep"][:], offs3)
             nc.sync.dma_start(lists["arr"][:], offs2)
@@ -164,6 +159,10 @@ def tile_list_parish_migration_pages_kernel(
             )
 
         pools["later"] = ctx.enter_context(tc.tile_pool(name="later", bufs=1))
+        gain_rows = sb("gain_rows", [P, P], F32)
+        late_sc = sb("late_sc", [P, KP, PASS], U8)
+        nc.vector.memset(gain_rows[:], 0.0)
+        nc.vector.memset(late_sc[:].rearrange("p a c -> p (a c)").bitcast(I32), 0)
         wd_pairs.append(sb("wd_pair1", [P, KP, 2 * WA_COLS], U8))
         wd_wide = sb("wd_wide", [P, KP, 2 * PASS], U8)
         wg = {kind: sb("wg_" + kind, [P, S], F32) for kind in ("arr", "dep")}
@@ -198,6 +197,8 @@ def tile_list_parish_migration_pages_kernel(
             pages[kind].append(sb(f"page_{kind}{len(pages[kind])}", [P, T2], F32, tag=tag))
             nc.gpsimd.memset(pages[kind][-1][:], 0.0)
 
+        pages["dep"].append(sb("first_page", [P, T2], F32))
+        nc.vector.memset(pages["dep"][0][:].bitcast(I32), 0)
         clear_page("dep", "picked_sc")
         wo_raw = [sb(f"wo_raw{g}", [P, PACK * N], F32, tag=f"big{g}") for g in range(RP)]
         nc.sync.dma_start(

@@ -249,12 +249,12 @@ def tile_list_parish_migration_pages_kernel(
         def deal_wd():
             wd_dealt = later("wd_dealt", [P, PACK * KP * 3 * P], U8, "stage0")
             nc.vector.tensor_copy(
-                wd_dealt[:, : PACK * KP * 2 * P].bitcast(I32).rearrange("p (t a c w) -> p a c t w", t=PACK, a=KP, w=2),
-                wd_wide[:].bitcast(I32).rearrange("p a (c t w) -> p a c t w", t=PACK, w=2),
+                wd_dealt[:, : PACK * KP * 2 * P].bitcast(I32).rearrange("p (t a c w) -> p t a c w", t=PACK, a=KP, w=2),
+                wd_wide[:].bitcast(I32).rearrange("p a (c t w) -> p t a c w", t=PACK, w=2),
             )
             nc.vector.tensor_copy(
-                wd_dealt[:, PACK * KP * 2 * P :].bitcast(I32).rearrange("p (t a c) -> p a c t", t=PACK, a=KP),
-                late_sc[:].bitcast(I32).rearrange("p a (c t) -> p a c t", t=PACK),
+                wd_dealt[:, PACK * KP * 2 * P :].bitcast(I32).rearrange("p (t a c) -> p t a c", t=PACK, a=KP),
+                late_sc[:].bitcast(I32).rearrange("p a (c t) -> p t a c", t=PACK),
             )
 
         def cast_wide(a):
@@ -273,10 +273,12 @@ def tile_list_parish_migration_pages_kernel(
 
         def cast_wo(g):
             wo_stage = later(f"wo_stage{g}", [P, PACK * N], BF16, ("wa_wide0", "wa_wide2")[g])
-            nc.scalar.copy(
-                wo_stage[:].rearrange("p (t m j) -> p m j t", t=PACK, j=PACK),
-                wo_raw[g][:].rearrange("p (j m t) -> p m j t", j=PACK, t=PACK),
-            )
+            for s in range(2):
+                lo = s * 2 * PACK * P
+                nc.scalar.copy(
+                    wo_stage[:, lo : lo + 2 * PACK * P].rearrange("p (t m j) -> p m j t", t=2, j=PACK),
+                    wo_raw[g][:].rearrange("p (j m t) -> p m j t", j=PACK, t=PACK)[:, :, :, 2 * s : 2 * s + 2],
+                )
 
         def quantize_wo(g):
             cols = slice(g * N, (g + 1) * N)

from contextlib import ExitStack

import concourse.mybir as mybir
from concourse.masks import make_identity

K, H, N, T, S, T2 = 1536, 1024, 512, 2048, 512, 1024
FLOPS = 2 * (2 * K * H * S + H * N * T2)

F32 = mybir.dt.float32
BF16 = mybir.dt.bfloat16
I32 = mybir.dt.int32
U32 = mybir.dt.uint32
U16 = mybir.dt.uint16
U8 = mybir.dt.uint8
E4M3 = mybir.dt.float8_e4m3fn_x4
E2M1 = mybir.dt.float4_e2m1fn_x4
ACT = mybir.ActivationFunctionType
MULT = mybir.AluOpType.mult
ADD = mybir.AluOpType.add

P = 128
PACK = 4
PASS = P * PACK
KP = K // PASS
RP = H // PASS
TILES = H // P
BANK = 512
HALVES = T2 // BANK
QUART = 256
CHUNKS = T2 // QUART
WA_COLS = 256
WA_CHUNKS = PASS // WA_COLS
SCALE_ROWS = 16
FIRST_TAGS = ("list", "big", "picked", "v_", "wd_sc", "wd_pair0", "ident", "gain_dealt")
RES_RING = 4
H_RING = 3
AHEAD = 2
OPEN_STEPS = (2, 3, 6, 7, 10, 11)
TIGHT_FROM = 9
SUM_STEPS = (5, 6, 8, 9, 12, 13)
GAIN_ON_VECTOR = (5, 6, 7, 9)
SUMMED = 6
WIDE_RING = 8
GAIN_RUN = 13
CAST_STEPS = (0, 8, 11)
WIDE_STEP = 4
NEEDS = {3: 1, 5: 3, 8: 5, 11: 9}
WEIGHED_FIRST = 1
QUANTIZE_STEPS = (1, 3, 9, 11, 13)
Z0_STEP = 11
DEAL_STEP = 5


def step_order():
    steps = [("dep", 0), ("dep", 1), ("dep", 2), ("arr", 0), ("arr", 1), ("dep", 3), ("arr", 2), ("arr", 3)]
    return steps + [("dep", 4), ("dep", 5), ("dep", 6), ("arr", 4), ("arr", 5), ("dep", 7), ("arr", 6), ("arr", 7)]


def tile_list_parish_migration_pages_kernel(
    tc, tab_words, tab_scales, offs, offs2, offs3, wa, wd_words, wd_scales,
    wg1, wg2, gain, res, wo, out_0, out_1, out_2,
):
    nc = tc.nc
    with ExitStack() as ctx:
        keep = ctx.enter_context(tc.tile_pool(name="keep", bufs=1))
        psum = ctx.enter_context(tc.psum_pool(name="psum", bufs=1))

        pools = {"first": keep}

        def sb(name, shape, dtype, tag=None):
            tag = tag or name
            pool = pools["first" if tag.startswith(FIRST_TAGS) else "later"]
            return pool.tile(shape, dtype, name=name, tag=tag, align_bytes=64)

        made = {}

        def later(name, shape, dtype, tag):
            if name not in made:
                made[name] = sb(name, shape, dtype, tag=tag)
            return made[name]

        banks = [psum.tile([P, BANK], F32, name=f"bank{b}") for b in range(8)]
        h_banks, sum_banks, word_banks = banks[0:2], banks[2:6], banks[6:8]

        list_t = sb("list_t", [P, S // 16], U16)
        lists = {"arr": sb("list_a", [P, S // 16], U16), "dep": sb("list_d", [P, S // 16], U16)}
        table = [sb(f"table{a}", [P, T], I32, tag=f"big{a}") for a in range(KP)]
        picked_sc = sb("picked_sc", [P, S], U8)
        v_sc = sb("v_sc", [P, KP, S], U8)
        wd_sc_raw = sb("wd_sc_raw", [P, KP, PASS], U8)
        wd_sc = sb("wd_sc", [P, KP * PASS], U8)
        wd_pairs = [sb("wd_pair0", [P, KP, 2 * WA_COLS], U8)]
        gain_dealt = sb("gain_dealt", [P, 16], F32)
        pages = {"dep": [], "arr": []}
        ident = sb("ident", [P, P], F32)

        def dealt(rows, t):
            return rows.rearrange("(c t i) w -> t c i w", t=PACK, i=PACK)[t]

        def load_wd(dst, lo, hi):
            cols = wd_words.rearrange("a p c -> p a c")[:, :, 2 * lo : 2 * hi]
            nc.sync.dma_start(out=dst[:].bitcast(I32), in_=cols.bitcast(I32))

        def load_wa(dst, a, lo, hi):
            nc.sync.dma_start(
                out=dst[:].rearrange("p (j c) -> p j c", j=PACK),
                in_=wa[a * PASS : (a + 1) * PASS, lo:hi].rearrange("(p j) c -> p j c", j=PACK),
            )

        def load_wg_dealt(kind, t):
            for q in (0, 2, 1, 3):
                nc.sync.dma_start(out=wg_dealt[kind][t][32 * q : 32 * q + 32, :], in_=dealt(wg1 if kind == "arr" else wg2, t))

        def load_res(i):
            rows = res[i * P : (i + 1) * P, :] if i < PACK else dealt(res[PASS:, :], i - PACK)
            nc.sync.dma_start(out=res_t[i][:], in_=rows)

        def load_table(a):
            nc.sync.dma_start(out=table[a][:], in_=tab_words[a].rearrange("p t i -> p (t i)").bitcast(I32))

        def load_scale_rows(queue, dst, src):
            rows = src.rearrange("a (q r) c -> r q a c", r=4)
            for r in range(4):
                queue.dma_start(out=dst[r:P:32, :, :].bitcast(I32), in_=rows[r].bitcast(I32))

        gain_view = gain[PASS:].rearrange("(c x) -> c x", x=16)

        def load_gain_dealt(i):
            nc.sync.dma_start(out=gain_dealt[i:P:PACK, 0:GAIN_RUN], in_=gain_view[:, i : i + GAIN_RUN])

        with tc.tile_pool(name="window", bufs=1) as window_pool:
            table_sc = window_pool.tile([P, T], U8, name="table_sc", align_bytes=64)
            nc.vector.memset(table_sc[:].bitcast(I32), 0)
            make_identity(nc, ident[:])
            nc.vector.memset(wd_sc[:].bitcast(I32), 0)
            nc.vector.memset(v_sc[:].rearrange("p a c -> p (a c)").bitcast(I32), 0)
            nc.sync.dma_start(list_t[:], offs)
            nc.sync.dma_start(lists["dep"][:], offs3)
            nc.sync.dma_start(lists["arr"][:], offs2)
            load_scale_rows(nc.sync, wd_sc_raw, wd_scales[:, :, :PASS])
            load_table(0)
            nc.scalar.dma_start(
                out=table_sc[0 : KP * SCALE_ROWS, :].bitcast(I32), in_=tab_scales.rearrange("a s t -> s a t").bitcast(I32)
            )
            for i in range(PACK):
                load_gain_dealt(i)
            load_table(1)
            load_wd(wd_pairs[0], 0, WA_COLS)
            load_table(2)
            for q in range(4):
                live = slice(32 * q, 32 * q + 4)
                nc.vector.tensor_copy(
                    wd_sc[live, :].bitcast(I32), wd_sc_raw[live, :, :].rearrange("p a c -> p (a c)").bitcast(I32)
                )
            nc.vector.tensor_copy(picked_sc[:], table_sc[:].indirect(list_t[:]))
        for q in range(4):
            nc.sync.dma_start(
                out=v_sc[32 * q : 32 * q + 4, :, :].bitcast(I32), in_=picked_sc[4 * KP * q : 4 * KP * (q + 1), :].bitcast(I32)
            )

        pools["later"] = ctx.enter_context(tc.tile_pool(name="later", bufs=1))
        gain_rows = sb("gain_rows", [P, P], F32)
        late_sc = sb("late_sc", [P, KP, PASS], U8)
        nc.vector.memset(gain_rows[:], 0.0)
        nc.vector.memset(late_sc[:].rearrange("p a c -> p (a c)").bitcast(I32), 0)
        wd_pairs.append(sb("wd_pair1", [P, KP, 2 * WA_COLS], U8))
        wd_wide = sb("wd_wide", [P, KP, 2 * PASS], U8)
        wg = {kind: sb("wg_" + kind, [P, S], F32) for kind in ("arr", "dep")}
        wg_dealt = {kind: [sb(f"wg_{kind}{t}", [P, S], F32) for t in range(PACK)] for kind in ("arr", "dep")}
        wa_raw = [[sb(f"wa_raw{c}_{a}", [P, PACK * WA_COLS], F32) for a in range(KP)] for c in range(WA_CHUNKS)]
        wa_wide = [sb(f"wa_wide{a}", [P, PACK * PASS], F32) for a in range(KP)]
        res_t = [sb(f"res{b}", [P, T2], F32) for b in range(RES_RING)]
        for a in range(KP):
            load_wa(wa_raw[0][a], a, 0, WA_COLS)
            if a == 0:
                nc.sync.dma_start(out=wg["dep"][:], in_=wg2)
        nc.sync.dma_start(out=gain_rows[0:PACK, :], in_=gain[0:PASS].rearrange("(i p) -> i p", p=P))
        load_wd(wd_pairs[1], WA_COLS, PASS)
        nc.sync.dma_start(out=wg["arr"][:], in_=wg1)
        for a in range(KP):
            load_wa(wa_raw[1][a], a, WA_COLS, PASS)
        load_res(0)
        load_wa(wa_wide[0], 0, PASS, H)
        load_res(1)
        load_wd(wd_wide, PASS, H)
        load_scale_rows(nc.sync, late_sc, wd_scales[:, :, PASS:])
        for a in range(1, KP):
            load_wa(wa_wide[a], a, PASS, H)
        load_res(2)
        load_res(3)

        v_words = [sb(f"v_words{a}", [P, S], U32) for a in range(KP)]
        for a in range(KP):
            nc.vector.tensor_copy(v_words[a][:], table[a][:].bitcast(U32).indirect(list_t[:]))

        def clear_page(kind, tag):
            pages[kind].append(sb(f"page_{kind}{len(pages[kind])}", [P, T2], F32, tag=tag))
            nc.gpsimd.memset(pages[kind][-1][:], 0.0)

        pages["dep"].append(sb("first_page", [P, T2], F32))
        nc.vector.memset(pages["dep"][0][:].bitcast(I32), 0)
        clear_page("dep", "picked_sc")
        wo_raw = [sb(f"wo_raw{g}", [P, PACK * N], F32, tag=f"big{g}") for g in range(RP)]
        nc.sync.dma_start(
            out=wo_raw[0][:].rearrange("p (j n) -> p j n", j=PACK), in_=wo[0:PASS, :].rearrange("(p j) n -> p j n", j=PACK)
        )
        load_wg_dealt("dep", 0)
        for t in range(PACK):
            nc.sync.dma_start(out=wo_raw[1][:, t * N : (t + 1) * N], in_=dealt(wo[PASS:, :], t))
        dealt_steps = [step for step in step_order() if step[1] >= PACK]
        for n, (kind, i) in enumerate(dealt_steps[1:]):
            load_wg_dealt(kind, i - PACK)
            if n < TILES - RES_RING:
                res_t.append(sb(f"res{RES_RING + n}", [P, T2], F32, tag=f"res{n}"))
                load_res(RES_RING + n)

        steps = step_order()
        last = len(steps) - 1
        where = {step: j for j, step in enumerate(steps)}
        stages = [sb(f"stage{c}", [P, KP * PACK * WA_COLS], BF16) for c in range(WA_CHUNKS)]
        wa_codes = [sb(f"wa_codes{c}", [P, KP * WA_COLS], U32) for c in range(WA_CHUNKS)]
        wa_sc = {}
        wide_codes = sb("wide_codes", [P, KP * PASS], U32)
        wide_sc = sb("wide_sc", [P, KP * PASS], U8)
        wo_codes = sb("wo_codes", [P, RP * N], U32)
        wo_sc = sb("wo_sc", [P, RP * N], U8)
        z_rows = [sb(f"z_rows{hb}", [P, 4, 2, 2 * P], BF16) for hb in range(HALVES)]
        z_in = sb("z_in", [P, PACK * T2], BF16)
        z_codes = [sb(f"z_codes{g}", [P, T2], U32) for g in range(RP)]
        z_sc = [None, sb("z_sc1", [P, T2], U8)]

        def cast_wa(c):
            for a in range(KP):
                nc.scalar.copy(
                    stages[c][:, a * PACK * WA_COLS : (a + 1) * PACK * WA_COLS].rearrange("p (c i j) -> p c j i", i=4, j=PACK),
                    wa_raw[c][a][:].rearrange("p (j c i) -> p c j i", i=4, j=PACK),
                )

        def quantize_wa(c):
            wa_sc[c] = sb(f"wa_sc{c}", [P, KP * WA_COLS], U8, tag=f"pin_wa{c}")
            width = KP * WA_COLS // 2
            for h in range(2):
                cols = slice(h * width, (h + 1) * width)
                nc.vector.quantize_mx(
                    out=wa_codes[c][:, cols].bitcast(E4M3), scales=wa_sc[c][:, cols],
                    in_=stages[c][:, PACK * h * width : PACK * (h + 1) * width],
                )

        def deal_wd():
            wd_dealt = later("wd_dealt", [P, PACK * KP * 3 * P], U8, "stage0")
            nc.vector.tensor_copy(
                wd_dealt[:, : PACK * KP * 2 * P].bitcast(I32).rearrange("p (t a c w) -> p t a c w", t=PACK, a=KP, w=2),
                wd_wide[:].bitcast(I32).rearrange("p a (c t w) -> p t a c w", t=PACK, w=2),
            )
            nc.vector.tensor_copy(
                wd_dealt[:, PACK * KP * 2 * P :].bitcast(I32).rearrange("p (t a c) -> p t a c", t=PACK, a=KP),
                late_sc[:].bitcast(I32).rearrange("p a (c t) -> p t a c", t=PACK),
            )

        def cast_wide(a):
            wide_stage = later("wide_stage", [P, KP * PACK * PASS], BF16, "pin_wide")
            nc.scalar.copy(
                wide_stage[:, a * PACK * PASS : (a + 1) * PACK * PASS].rearrange("p (t c i j) -> p c t j i", t=PACK, i=PACK, j=PACK),
                wa_wide[a][:].rearrange("p (j c t i) -> p c t j i", j=PACK, t=PACK, i=PACK),
            )

        def quantize_wide():
            for lo, hi in ((0, 2 * PASS), (2 * PASS, KP * PASS)):
                nc.vector.quantize_mx(
                    out=wide_codes[:, lo:hi].bitcast(E4M3), scales=wide_sc[:, lo:hi],
                    in_=made["wide_stage"][:, PACK * lo : PACK * hi],
                )

        def cast_wo(g):
            wo_stage = later(f"wo_stage{g}", [P, PACK * N], BF16, ("wa_wide0", "wa_wide2")[g])
            for s in range(2):
                lo = s * 2 * PACK * P
                nc.scalar.copy(
                    wo_stage[:, lo : lo + 2 * PACK * P].rearrange("p (t m j) -> p m j t", t=2, j=PACK),
                    wo_raw[g][:].rearrange("p (j m t) -> p m j t", j=PACK, t=PACK)[:, :, :, 2 * s : 2 * s + 2],
                )

        def quantize_wo(g):
            cols = slice(g * N, (g + 1) * N)
            nc.vector.quantize_mx(out=wo_codes[:, cols].bitcast(E4M3), scales=wo_sc[:, cols], in_=made[f"wo_stage{g}"][:])

        def h_tile(j):
            return later(f"h_step{j}", [P, S], F32, {Z0_STEP - 1: "pin_z", WIDE_STEP - 1: "pin_wide", 0: "pin_wa0", 2: "pin_wa1", 5: "stage1"}.get(j, f"h{j % H_RING}"))

        silu_tags = {
            0: "wa_raw0_2", 1: "wa_raw1_2", 2: "silu_spare", 3: "wa_raw0_0", 4: "wa_raw1_0", 5: "wa_raw1_1",
            6: "big2", 7: "wd_sc_raw", 8: "wa_wide2", 15: "wa_wide1",
        }
        silu_again = {9: 5, 11: 0, 10: 1, 12: 2, 13: 3, 14: 4}

        def silu_tile(j):
            j = silu_again.get(j, j)
            return later(f"silu_step{j}", [P, T2], F32, silu_tags[j])

        def page_of(j):
            kind, i = steps[j]
            return pages[kind][(i + ((kind, i) == ("dep", 3))) % 2]

        def gain_col(i):
            return gain_t[:, i : i + 1] if i < PACK else gain_dealt[:, PACK * (i - PACK) : PACK * (i - PACK) + 1]

        def z_words():
            return later("z_words", [P, PACK * T2], BF16, "wa_wide0")

        def product(j):
            kind, i = steps[j]
            bank = (h_banks + word_banks)[j % 4] if j < WIDE_RING else h_banks[j % 2]
            for a in range(KP):
                t = i - PACK
                if kind == "arr" and i < PACK:
                    c, col = divmod(i * P, WA_COLS)
                    cols = slice(a * WA_COLS + col, a * WA_COLS + col + P)
                    lhs, lhs_sc = wa_codes[c][:, cols].bitcast(E4M3), wa_sc[c][:, cols]
                elif kind == "arr":
                    cols = slice(a * PASS + t * P, a * PASS + (t + 1) * P)
                    lhs, lhs_sc = wide_codes[:, cols].bitcast(E4M3), wide_sc[:, cols]
                elif i < PACK:
                    lhs = wd_pairs[i // 2][:, a, (i % 2) * 2 * P : (i % 2 + 1) * 2 * P].bitcast(E2M1)
                    lhs_sc = wd_sc[:, a * PASS + i * P : a * PASS + (i + 1) * P]
                else:
                    n = t * KP + a
                    lhs = made["wd_dealt"][:, n * 2 * P : (n + 1) * 2 * P].bitcast(E2M1)
                    lhs_sc = made["wd_dealt"][:, (2 * PACK * KP + n) * P : (2 * PACK * KP + n + 1) * P]
                nc.tensor.matmul_mx(
                    out=bank[:], lhsT=lhs, lhsT_scale=lhs_sc, rhs=v_words[a][:].bitcast(E4M3),
                    rhs_scale=v_sc[:, a, :], start=(a == 0), stop=(a == KP - 1),
                )
            if j < WEIGHED_FIRST:
                nc.vector.tensor_tensor(h_tile(j)[:], bank[:], wg[kind][:], MULT)
            else:
                nc.scalar.copy(h_tile(j)[:], bank[:])

        def scatter(j):
            kind, i = steps[j]
            window = page_of(j)[:].indirect(lists[kind][:])
            if j < WEIGHED_FIRST:
                nc.vector.tensor_copy(window, h_tile(j)[:])
            else:
                nc.vector.tensor_tensor(window, h_tile(j)[:], (wg[kind] if i < PACK else wg_dealt[kind][i - PACK])[:], MULT)

        halves = [slice(hb * BANK, (hb + 1) * BANK) for hb in range(HALVES)]

        def activate(j):
            kind, i = steps[j]
            tile = silu_tile(j)
            if i >= SUMMED or j in GAIN_ON_VECTOR:
                nc.scalar.activation(tile[:], page_of(j)[:], ACT.Silu)
                return
            parts = halves if i >= PACK and kind == "arr" else [slice(0, T2)]
            for cols in parts:
                nc.scalar.activation(tile[:, cols], page_of(j)[:, cols], ACT.Silu)
            for cols in parts:
                nc.scalar.activation(tile[:, cols], tile[:, cols], ACT.Copy, scale=gain_col(i))

        def combine(j):
            kind, i = steps[j]
            tile = silu_tile(j)
            if j in GAIN_ON_VECTOR:
                nc.vector.tensor_scalar(tile[:], tile[:], gain_col(i), None, MULT)
            elif kind == "dep" and i >= SUMMED:
                nc.vector.scalar_tensor_tensor(tile[:], tile[:], gain_col(i), res_t[i][:], MULT, ADD)

        def add_term(i, hb, src, first, final):
            for n in range(4):
                m0 = (4 * hb + n) * P
                if i < PACK:
                    bank, b = sum_banks[2 * (i % 2) + hb], n
                else:
                    bank, b = sum_banks[2 * hb + n // 2], 2 * (i - PACK) + n % 2
                nc.tensor.matmul(
                    bank[:, b * P : (b + 1) * P], src[:, m0 : m0 + P], ident[:],
                    start=(first and b == 0), stop=(final and b == 3), is_transpose=True,
                )

        def round_sum(i, hb):
            if i >= PACK:
                pairs = later("z_pairs", [P, T2 * 2], BF16, "wa_wide1")
                for k in range(2 * hb, 2 * hb + 2):
                    nc.scalar.copy(
                        pairs[:, k * BANK : (k + 1) * BANK].rearrange("p (w e) -> p w e", e=2),
                        sum_banks[k][:].rearrange("p (e w) -> p w e", e=2),
                    )
                return
            nc.scalar.copy(
                z_rows[hb][:, :, :, 64 * i : 64 * (i + 1)].rearrange("p b u (q e) -> p b u q e", e=2),
                sum_banks[2 * (i % 2) + hb][:].rearrange("p (b q u e) -> p b u q e", b=4, u=2, e=2),
            )

        def interleave_z(q, bank):
            hb, pair = divmod(q, 2)
            words = z_rows[hb][:].bitcast(F32)
            for b in range(2):
                for u in range(2):
                    col = (2 * b + u) * P
                    nc.tensor.transpose(bank[:, col : col + P], words[:, 2 * pair + b, u, :], ident[:])
            nc.scalar.copy(
                z_in[:].bitcast(F32)[:, q * BANK : (q + 1) * BANK].rearrange("p (b m u) -> p b m u", b=2, u=2),
                bank[:].rearrange("p (b u m) -> p b m u", b=2, u=2),
            )

        def weave(q):
            blocks = z_words()[:].bitcast(F32).rearrange("p (n m) -> p n m", m=QUART)
            second = CHUNKS + q % 2
            nc.vector.tensor_copy(
                z_in[:].bitcast(F32)[:, 2 * q * QUART : 2 * (q + 1) * QUART].rearrange("p (m u) -> p m u", u=2),
                blocks[:, q : second + 1 : second - q, :].rearrange("p u m -> p m u"),
            )

        def quantize_z(g, lo, hi):
            nc.vector.quantize_mx(
                out=z_codes[g][:, lo:hi].bitcast(E4M3), scales=z_sc[g][:, lo:hi], in_=z_in[:, PACK * lo : PACK * hi]
            )

        y_banks = [banks[2:4], banks[4:6], banks[6:8], banks[0:2]]

        def y_pass(g, q):
            cols = slice(q * QUART, (q + 1) * QUART)
            for t in range(PACK):
                w = slice(g * N + t * P, g * N + (t + 1) * P)
                nc.tensor.matmul_mx(
                    out=y_banks[q][t // 2][:, (t % 2) * QUART : (t % 2 + 1) * QUART],
                    lhsT=wo_codes[:, w].bitcast(E4M3), lhsT_scale=wo_sc[:, w],
                    rhs=z_codes[g][:, cols].bitcast(E4M3), rhs_scale=z_sc[g][:, cols],
                    start=(g == 0 and t % 2 == 0), stop=(g == RP - 1 and t % 2 == 1),
                )

        def open_sum(i):
            for hb in range(HALVES):
                add_term(i, hb, res_t[i], i <= PACK, False)
                add_term(i, hb, silu_tile(where[("dep", i)]), False, False)

        def finish_sum(i):
            for hb in range(HALVES):
                add_term(i, hb, silu_tile(where[("arr", i)]), False, i != PACK)
                if i != PACK:
                    round_sum(i, hb)
            if i == PACK - 1:
                for q in range(CHUNKS):
                    interleave_z(q, word_banks[q % 2])
            if i == SUMMED - 1:
                words = made["z_pairs"][:].bitcast(F32)
                for hb in range(HALVES):
                    for b in range(4):
                        m0 = (4 * hb + b) * P
                        nc.tensor.transpose(word_banks[hb][:, b * P : (b + 1) * P], words[:, m0 : m0 + P], ident[:])
                    nc.scalar.copy(z_words()[:].bitcast(F32)[:, hb * BANK : (hb + 1) * BANK], word_banks[hb][:])

        issued = [2]
        casts = (lambda: cast_wa(1), lambda: cast_wo(0), lambda: cast_wo(1))
        quantizers = (
            lambda: quantize_wa(0), lambda: quantize_wa(1), quantize_wide,
            lambda: quantize_wo(0), lambda: quantize_wo(1),
        )
        def products_up_to(j):
            for ahead in range(issued[0], min(j + AHEAD, last) + 1):
                if j < NEEDS.get(ahead, 0):
                    break
                product(ahead)
                issued[0] = ahead + 1

        cast_wa(0)
        product(0)
        product(1)
        gain_t = sb("gain_t", [P, PACK], F32, tag="wa_raw0_1")
        nc.tensor.transpose(h_banks[0][:, 0:P], gain_rows[:], ident[:])
        nc.scalar.copy(gain_t[:], h_banks[0][:, 0:PACK])
        clear_page("arr", "wd_pair0")
        clear_page("arr", "gain_rows")
        for j in range(last):
            scatter(j)
            if j in QUANTIZE_STEPS:
                quantizers[QUANTIZE_STEPS.index(j)]()
            if j == Z0_STEP:
                z_sc[0] = sb("z_sc0", [P, T2], U8, tag="pin_z")
                quantize_z(0, 0, T2)
            if j == DEAL_STEP:
                deal_wd()
            if j > 0:
                combine(j - 1)
            if j < TIGHT_FROM:
                products_up_to(j)
            activate(j)
            products_up_to(j)
            if j in CAST_STEPS:
                casts[CAST_STEPS.index(j)]()
            if WIDE_STEP <= j < WIDE_STEP + KP:
                cast_wide(j - WIDE_STEP)
            if j in SUM_STEPS:
                finish_sum(SUM_STEPS.index(j))
            if j in OPEN_STEPS:
                open_sum(OPEN_STEPS.index(j))

        for q in (0, 1, 3, 2):
            y_pass(0, q)
        scatter(last)
        i = TILES - 1
        mine = silu_tile(last)
        quarters = [slice(q * QUART, (q + 1) * QUART) for q in range(CHUNKS)]
        for cols in quarters:
            nc.scalar.activation(mine[:, cols], page_of(last)[:, cols], ACT.Silu)
        for q, cols in enumerate(quarters):
            for n in (i - 1, i):
                arr, dep = silu_tile(where[("arr", n)]), silu_tile(where[("dep", n)])
                lo = 2 * (CHUNKS + q % 2) * QUART
                pair = z_words()[:, lo : lo + 2 * QUART].rearrange("p (m e) -> p e m", e=2)[:, n - SUMMED, :]
                nc.vector.scalar_tensor_tensor(pair, arr[:, cols], gain_col(n), dep[:, cols], MULT, ADD)
            weave(q)
            quantize_z(1, q * QUART, (q + 1) * QUART)
            y_pass(1, q)
        y_view = out_0.rearrange("(p t) m -> p t m", t=PACK)
        codes_view = out_1[0].rearrange("p m t -> p (m t)").bitcast(I32)
        y_sc = sb("y_sc", [P, T2], U8)
        y_codes = [sb(f"y_codes{q}", [P, QUART], U32) for q in range(CHUNKS)]
        y_sb = [sb(f"y_sb{h}", [P, 2 * PACK * QUART], F32, tag=("wa_wide2", "big0")[h]) for h in range(2)]
        for q in range(CHUNKS):
            cols = slice(q * QUART, (q + 1) * QUART)
            rows = y_sb[q // 2][:, (q % 2) * PACK * QUART : (q % 2 + 1) * PACK * QUART]
            rounded = z_rows[q // 2][:].rearrange("p b u w -> p (b u w)")[:, (q % 2) * PACK * QUART : (q % 2 + 1) * PACK * QUART]
            for s in range(2):
                half = rows[:, s * BANK : (s + 1) * BANK]
                nc.scalar.copy(half, y_banks[q][s][:])
                nc.sync.dma_start(out=y_view[:, 2 * s : 2 * s + 2, cols], in_=half.rearrange("p (t m) -> p t m", t=2))
            nc.vector.tensor_copy(
                rounded.rearrange("p (c i t) -> p c t i", i=PACK, t=PACK),
                rows.rearrange("p (t c i) -> p c t i", i=PACK, t=PACK),
            )
            nc.vector.quantize_mx(out=y_codes[q][:].bitcast(E4M3), scales=y_sc[:, cols], in_=rounded)
            nc.sync.dma_start(out=codes_view[:, cols], in_=y_codes[q][:].bitcast(I32))
        for q in range(4):
            queue = nc.sync if q % 2 == 0 else nc.scalar
            queue.dma_start(
                out=out_2[0, 4 * q : 4 * q + 4, :].bitcast(I32), in_=y_sc[32 * q : 32 * q + 4, :].bitcast(I32)
            )
